import numpy as np, ml_dtypes
CORES = [16,17,18,19,32,33,34,35]
N = 8
import mx_ref
BF = ml_dtypes.bfloat16
def gcols(t, e):
    v = np.concatenate([t.reshape(8, 16, -1, 4), np.zeros((8, 16, 1, 4), BF)], axis=2)
    return np.ascontiguousarray(np.stack([v[g][:, e[g]] for g in range(8)])).reshape(128, -1)
def tile(rs):
    return np.stack(rs, axis=2).reshape(128, -1).astype(BF)
def pick(q, e):
    c = np.concatenate([q[0].reshape(128, -1, 4), np.zeros((128, 1, 4), np.uint8)], axis=1); s = np.concatenate([q[1], np.ones((16, 1), np.uint8)], axis=1)
    return (np.ascontiguousarray(c[:, e].reshape(128, -1)), np.ascontiguousarray(s[:, e]))
def join(*qs):
    return (np.concatenate([q[0] for q in qs], axis=1), np.concatenate([q[1] for q in qs], axis=1))
def put(q, e, v):
    c, s = q[0].reshape(128, -1, 4).copy(), q[1].copy(); c[:, e] = v[0].reshape(128, -1, 4); s[:, e] = v[1]
    return (c.reshape(128, -1), s)
def pk(c, s):
    return (np.ascontiguousarray(c), mx_ref.live(s))
def emit(q):
    return q[0], q[1]
def packed(v, rng):
    q = [mx_ref.quantize(np.ascontiguousarray(v[r])) for r in range(N)]
    return np.stack([a for a, b in q]), np.stack([mx_ref.plane(b, rng) for a, b in q])
def values_of_codes():
    e, c = np.zeros((128, 128, 4), np.float32), np.zeros((128, 2, 4), np.uint8)
    e[np.arange(128), np.arange(128), 0] = 1
    c[:127, :, 0] = np.arange(256).reshape(2, 128).T[:127]
    return mx_ref.matmul(mx_ref.quantize(e.reshape(128, 512).astype(BF)), (c.reshape(128, 8), np.full((16, 2), 127, np.uint8))).T.reshape(-1).astype(np.float64)
CODE_VALUE, SCALE_VALUE = values_of_codes(), 2.0 ** (np.arange(256) - 127.0)
def decode(q):
    return (CODE_VALUE[q[0]].reshape(16, 8, -1, 4) * SCALE_VALUE[q[1]][:, None, :, None] + 0.0).reshape(128, -1).astype(np.float32)
def f(rng, *shape):
    return mx_ref.flush((rng.standard_normal(shape, dtype=np.float32) * np.exp2(rng.integers(-2, 3, shape[:-1] + (1,)))).astype(BF))
def wide(rng, *shape, cols=0):
    v = rng.standard_normal(shape, dtype=np.float32) * np.exp2(rng.integers(-12, 13, shape)).astype(np.float32)
    if cols: v *= np.repeat(np.exp2(rng.integers(-cols, cols + 1, shape[:-2] + (1, shape[-1] // 4))) * (rng.random(shape[:-2] + (1, shape[-1] // 4)) > 0.0625), 4, axis=-1).astype(np.float32)
    return mx_ref.flush(v.astype(BF))
C, B, K, R = 256, 16, 96, 3
def numbers_of(rng):
    return {"x": np.array(f(rng, N, 128, 4 * C)), "u": np.array(f(rng, N, 128, 512)), "v": np.array(f(rng, N, 128, 512))}
def layers(rng):
    return np.array(f(rng, N, 128, 2048)).reshape(N, 8, 16, 4, 8, 16, 4)
def weights(rng, w):
    c, p = packed(np.ascontiguousarray(w).reshape(N, 128, 2048), rng)
    return {"wc": c, "ws": p}
def lone(u, k, k2=0.0):
    a = u.reshape(N, 128, 128, 4)
    a[:, :, ::16] = 0
    for h in range(0, 128, 16):
        a[:, h, h, 0] = np.asarray(k, np.float32).astype(BF)
        a[:, h + 1, h, 0] = np.asarray(k2, np.float32).astype(BF)
    return a.reshape(N, 128, 512)
def setup_inputs(rng):
    return {**numbers_of(rng), **weights(rng, layers(rng))}
def setup_inputs_ties(rng):
    d = numbers_of(rng)
    m = C // B
    k = (rng.permutation(m) % 5)[:, None]
    one = 1 << rng.integers(0, 8, (N // 2, 2, m, B))
    two = one | (1 << rng.integers(0, 8, one.shape))
    w = np.where(k == 0, one * rng.integers(0, 2, one.shape), np.where(k == 3, two, 0))
    each = 1 << (np.arange(B) % 8)
    w[:, 0] += np.where(k == 2, each, 0)
    w[:, 1] += np.where(k == 4, each, 0)
    w = (w ^ rng.integers(0, 256, 4)[rng.integers(0, 4, (N // 2, 1, m, 1))]).reshape(N, 1, C)
    x = np.zeros((N, 8, 16, C, 4), np.float32)
    x[:, :, 0, :, 0] = ((w >> np.arange(8)[:, None]) & 1) * 2.0 - 1.0
    z = (N, 8, 8, C, 4)
    x[:, :, 8:] = (1.0 + (2 * rng.integers(0, 64, z) + 1) * 2.0 ** -7) * np.exp2(-rng.integers(2, 9, z)) * (rng.integers(0, 2, z) * 2.0 - 1.0)
    x[:, :, 8, :, 0] = 126.0 * (rng.integers(0, 2, (N, 8, C)) * 2.0 - 1.0)
    a = layers(rng)
    a[:, :, :, :, :, :8] = 0
    a[:, :, :, :, rng.permutation(8)[:4]] = 0
    return {"x": x.reshape(N, 128, 4 * C).astype(BF), "u": lone(d["u"], 1.0), "v": d["v"], **weights(rng, a)}
def setup_inputs_near(rng):
    d = numbers_of(rng)
    x = d["x"].reshape(N, 8, 16, C, 4)
    o = np.repeat(rng.permutation(N // 2) % 2, 2)
    small = (o == 0)[:, None, None]
    s = np.where(small, rng.choice([1.125, 2.0, -40.0, -40.0], (N, 8, C)) * 2.0 ** -30, rng.integers(-1, 2, (N, 8, C)))
    less = np.where(small, -1.25 * 2.0 ** -30, np.zeros((N, 8, C)))
    for r in range(N):
        for g in rng.permutation(8)[:4]:
            c = rng.integers(C)
            s[r, g, c] = 2.0 ** 29
            less[r, g, c] = 2.0 ** 29
    x[:, :, :8] = 0
    x[:, :, 0, :, 0] = s.astype(np.float32).astype(BF)
    x[:, :, 1, :, 0] = less.astype(np.float32).astype(BF)
    w = layers(rng)
    w[:, :, :8] = 0
    w[:, :, :, :, :, :8] = 0
    return {"x": x.reshape(N, 128, 4 * C), "u": lone(d["u"], np.where(o == 0, 1.125 * 2.0 ** -30, 1.0), np.where(o == 0, 2.0 ** -30, 1.0)), "v": d["v"], **weights(rng, w)}
def setup_inputs_late(rng):
    d = numbers_of(rng)
    x = d["x"].reshape(N, 8, 16, C, 4)
    p = rng.permutation(N // 2)
    c = rng.choice([-1.0, 1.0]) * (1.0 - 2.0 * (p // 2 % 2))
    s = np.stack([c, np.where(p % 2 == 0, c, -c)], axis=1).reshape(N)
    x[:, :, 0] = s.astype(np.float32).astype(BF)[:, None, None, None]
    z = (N, 8, C, 4)
    a = (1.0 + (2 * rng.integers(0, 64, z) + 1) * 2.0 ** -7) * np.exp2(-rng.integers(13, 15, z))
    a[:, 0, :, 0] = 1.96875
    x[:, 7, 8:] = (a * (rng.integers(0, 2, z) * 2.0 - 1.0)).astype(np.float32).astype(BF)
    x[:, 6, 8:] = 0
    w = layers(rng)
    w[:, :, :, :, 6:, 8:] = 0
    for i in range(8, 16):
        for b in range(4): w[:, 7, i, b, 6, i, b] = 32
    w[:, 7, 8, 0, 6, 8, 0] = 0
    return {"x": x.reshape(N, 128, 4 * C), "u": lone(d["u"], 1.0), "v": d["v"], **weights(rng, w)}
def setup_inputs_ends(rng):
    d = numbers_of(rng)
    x = np.zeros((N, 8, 16, C, 4), np.float32)
    u = d["u"].reshape(N, 8, 16, 128, 4)
    u[:, :, :, ::16] = 0
    w = np.zeros((N, 128, 4, 128, 4), np.float32)
    i = np.arange(128)
    o = rng.permutation(N // 2) % 2
    for p in range(N // 2):
        e = slice(2 * p, 2 * p + 2)
        k = 2.0 ** 30 if o[p] == 0 else 2.0 ** -30
        for g in range(8): u[e, g, :, 16 * g] = k
        if o[p] == 0:
            c = rng.choice([-1.0, 1.0], (C // B, 1)) * np.ones((1, 8))
            h = np.argsort(rng.random(c.shape), axis=1)[:, :2]
            np.put_along_axis(c, h, -c[:, :2], axis=1)
            m = rng.permutation(C // B)[:2]
            c[m[0]], c[m[1]] = 1.0, -1.0
            s = 0.75 + 0.25 * rng.random((2, 8, 16, C, 4))
            for a in m: s[:, :, :, B * a:B * a + B] = 1.0
            x[e] = 2.0 ** 30 * s * np.repeat(c.T, B, axis=1)[:, None, :, None]
            for g in rng.permutation(8)[:4]: u[e, :, :, 16 * g] = k
            d["v"][e] = (2.0 ** 30 * rng.choice([-1.0, 1.0], (2, 128, 512))).astype(np.float32).astype(BF)
            for b in range(4): w[e, i, b, i, b] = -1
        else:
            x[e] = 2.0 ** -30
            for g in range(8): x[2 * p + 1, g][:, np.arange(C) % B % 8 == g] = -7.0 * 2.0 ** -30
    d["v"] = (np.where(d["v"] < 0, -1.0, 1.0) * np.where(rng.permutation(N) % 2, 2.0 ** -30, 2.0 ** 30)[:, None, None]).astype(np.float32).astype(BF)
    return {"x": x.reshape(N, 128, 4 * C).astype(BF), "u": u.reshape(N, 128, 512), "v": d["v"], **weights(rng, w.astype(BF))}
def setup_inputs_spread(rng):
    d = setup_inputs(rng)
    d["x"] = wide(rng, N, 128, 4 * C, cols=6)
    return d
def check_inputs(d):
    b = []
    for k in ("x", "u", "v"):
        a = np.abs(d[k].astype(np.float32))
        if not (np.isfinite(a).all() and ((a == 0) | (a >= 2.0 ** -30) & (a <= 2.0 ** 30)).all()): b.append("a value of " + k)
    none, least, most = [emit(mx_ref.quantize(np.full((128, 16), k, np.float32).astype(BF)))[1][0, 0] for k in (0.0, 2.0 ** -30, 2.0 ** 30)]
    for r in range(N):
        if ((d["wc"][r] == 0x7F) | (d["wc"][r] == 0xFF)).any(): b.append("wc: a code that is no number")
        s = mx_ref.live(d["ws"][r])
        if ((s != none) & ((s < least) | (s > most))).any(): b.append("ws: a scale out of range")
    return b
def reference(x, u, v, wc, ws):
    qu = [mx_ref.quantize(u[r]) for r in range(N)]
    lay = [pk(wc[r], ws[r]) for r in range(N)]
    now = [x[r] for r in range(N)]
    mate = np.arange(N) ^ 1
    after = (np.arange(C)[:, None] + np.arange(1, C)) % C
    for t in range(R):
        q = [mx_ref.quantize(now[r]) for r in range(N)]
        own = [decode(q[r]).astype(BF) for r in range(N)]
        word = np.stack([np.packbits(mx_ref.matmul(qu[r], q[r])[::16] > 0, axis=0, bitorder="little")[0] for r in range(N)])
        theirs = word[:, :, None] ^ np.repeat(word[mate].reshape(N, -1, B), B, axis=1)
        ours = word[:, :, None] ^ word[:, after]
        care = np.full((N, C), 255, np.uint8)
        a, kept = np.zeros((N, 8, C), np.int64), np.zeros((N, 8, C), np.int64)
        for k in range(8):
            g = (3 * t + k) % 8
            bit = np.uint8(1 << g)
            keep = np.any((theirs & care[:, :, None]) == bit, axis=2)
            hit = (ours & care[:, :, None]) == bit
            first = after[np.arange(C), np.argmax(hit, axis=2)]
            a[:, g] = np.where(~keep & np.any(hit, axis=2), first, np.arange(C))
            kept[:, g] = keep
            care = np.where(keep, care, care & np.uint8(255 - (1 << g)))
        l = np.argsort(kept, axis=2, kind="stable")[:, :, :K]
        z = [((own[r].astype(np.float32) + gcols(own[r], a[r]).astype(np.float32)) * np.float32(0.5)).astype(BF) for r in range(N)]
        sent = [mx_ref.quantize(gcols(z[r], l[r])) for r in range(N)]
        now = []
        for r in range(N):
            came = sent[mate[r]]
            held = decode(came)
            made = tile([mx_ref.matmul(pick(lay[r], np.arange(128 * b, 128 * b + 128)), came) * np.float32(0.03125) + held[:, b::4] for b in range(4)]).reshape(8, 16, K, 4)
            new = z[r].reshape(8, 16, C, 4).copy()
            for g in range(8): new[g][:, l[r, g]] = made[g]
            now.append(new.reshape(128, 4 * C))
    y, al = np.zeros((N, 128, C), np.float32), np.zeros((N, 8, C + K), np.float32)
    oc, osc = np.zeros((N, 128, 4 * C), np.uint8), np.zeros((N, 16, C), np.uint8)
    for r in range(N):
        q = mx_ref.quantize(now[r])
        y[r] = mx_ref.matmul(mx_ref.quantize(v[r]), q)
        al[r] = np.concatenate([a[r], l[r]], axis=1)
        oc[r], osc[r] = emit(q)
    return {"y": y, "al": al, "oc": oc, "osc": osc}

@@ -1,0 +1,508 @@
+from concourse.bass import IndirectOffsetOnAxis
+from concourse.mybir import dt, AluOpType, AxisListType, ActivationFunctionType
+
+F32, BF, I32, U16, F8, U8 = "float32", "bfloat16", "int32", "uint16", "float8_e4m3fn_x4", "uint8"
+SCRATCH = {}
+for _n, _w, _d in [
+        ("X0", 1024, BF), ("UT", 512, BF), ("VT", 512, BF), ("WQ", 512, F8), ("WS", 512, U8),
+        ("UQ", 128, F8), ("US", 128, U8), ("VQ", 128, F8), ("VS", 128, U8), ("URQ", 384, F8), ("URS", 384, U8),
+        ("EHT", 2048, BF), ("EHQ", 512, F8), ("EHS", 512, U8), ("ELT", 2048, BF), ("ELQ", 512, F8), ("ELS", 512, U8),
+        ("CMT", 1024, BF), ("CMQ", 256, F8), ("CMS", 256, U8), ("COT", 1024, BF), ("COQ", 256, F8), ("COS", 256, U8),
+        ("HMT", 2048, BF), ("HMQ", 512, F8), ("HMS", 512, U8), ("MTT", 1024, BF), ("MTQ", 256, F8), ("MTS", 256, U8),
+        ("ICOL", 512, F32), ("VB", 256, BF), ("I8", 128, F32), ("I16", 128, F32), ("JP", 256, F32), ("TH", 128, F32),
+        ("IP", 10, I32), ("SC", 16, F32), ("UI", 24, I32), ("UL", 24, U16), ("PLF", 16, F32), ("PL", 16, U16),
+        ("ILF", 64, F32), ("IL", 32, U16), ("NI", 48, I32), ("NS", 16, F32),
+        ("EQT", 1056, BF), ("TB", 1568, BF), ("TK", 16, F32), ("H25", 256, BF), ("H50", 16, F32), ("H10", 96, F32),
+        ("H8", 16, F32), ("NEG", 512, F32), ("JC", 32, F32), ("JL", 32, F32), ("MK", 96, F32),
+        ("XQ", 256, F8), ("XS", 256, U8), ("XT", 1024, BF), ("BT", 768, BF), ("BQ", 192, F8), ("BS", 192, U8),
+        ("W8", 32, F32), ("PB", 32, F32), ("IX", 2, I32), ("SG", 48, F32), ("RS", 1568, BF),
+        ("OT", 1024, BF), ("OQ", 256, F8), ("OS", 256, U8), ("DS", 1024, F32), ("DT", 1024, BF), ("DQ", 256, F8), ("DP", 256, U8),
+        ("HI", 192, BF), ("E", 256, BF), ("XH", 256, F32), ("GS", 64, F32), ("TM", 32, F32),
+        ("RP", 16, F32), ("KK", 96, F32), ("AL", 24, F32), ("INC", 512, F32), ("O", 512, F32), ("XO", 4096, F32),
+        ("YI", 64, I32), ("YT", 64, F32),
+        ("LF", 192, F32), ("DL", 64, F32), ("AF", 64, F32), ("WC", 160, F32), ("AU", 16, U16), ("PU", 16, U16), ("LU", 8, U16), ("SU", 16, U16),
+        ("LR", 256, F32), ("LM", 192, F32), ("HP", 2048, BF), ("XW", 1408, BF), ("ET", 512, BF), ("YO", 256, F32)]:
+    SCRATCH[_n] = ("sbuf", [128, _w], _d)
+for _t in range(3):
+    SCRATCH["MS%d" % _t] = ("sbuf", [128, 64], BF)
+    SCRATCH["WL%d" % _t] = ("sbuf", [128, 64], BF)
+    SCRATCH["LB%d" % _t] = ("sbuf", [128, 16], F32)
+    SCRATCH["AC%d" % _t] = ("sbuf", [128, 128], F8)
+    SCRATCH["AS%d" % _t] = ("sbuf", [128, 128], U8)
+    if _t == 0:
+        SCRATCH["EQ"] = ("sbuf", [128, 128], F8)
+        SCRATCH["ES"] = ("sbuf", [128, 128], U8)
+for _b in range(8):
+    SCRATCH["B%d" % _b] = ("psum", [128, 512], F32)
+SCRATCH["tab"] = ("dram", [256, 784], BF)
+SEMAPHORES = ["cV", "cA", "cP", "cG", "dx", "du", "dv", "dw", "dtab", "dfill", "dout"]
+for _t in range(3):
+    SEMAPHORES += ["wa%d" % _t, "ca%d" % _t, "lw%d" % _t, "lc%d" % _t, "dl%d" % _t, "di%d" % _t]
+
+
+def rank_program(g, core, T, topo):
+    rank = T.rank_of(core)
+    if rank is None:
+        return
+    mate = T.cores[rank + 1 if rank % 2 == 0 else rank - 1]
+    A, AF = AluOpType, ActivationFunctionType
+    X = AxisListType.X
+    Q = {"V": g.vector, "A": g.scalar, "P": g.tensor, "G": g, "Y": g.sync}
+    own = {"V": "cV", "A": "cA", "P": "cP", "G": "cG", "Y": None}
+    tot, lastw, readers, epoch, known = {}, {}, {}, {}, {e: {} for e in Q}
+
+    def need(e, toks):
+        for s, v in sorted(toks):
+            n = tot[s] if v is None else v
+            if known[e].get(s, 0) < n:
+                Q[e].wait_ge(T.sem[s], n)
+                known[e][s] = n
+
+    def deps(e, r, w, add, compute):
+        toks = {}
+
+        def put(tk, war=False):
+            s, v = tk
+            if war and compute and s == own[e]:
+                return
+            n = tot[s] if v is None else v
+            toks[s] = max(toks.get(s, 0), n)
+        for k in r:
+            for tk in lastw.get(k, []):
+                put(tk)
+            if k[0] == "B" and k[1:].isdigit():
+                for tk in readers.get(k, []):
+                    put(tk, True)
+        for k in w:
+            for tk in lastw.get(k, []):
+                put(tk)
+            for tk in readers.get(k, []):
+                put(tk, True)
+        for k in add:
+            if readers.get(k):
+                epoch[k] = lastw.get(k, []) + readers[k]
+                lastw[k], readers[k] = [], []
+            for tk in epoch.get(k, []):
+                put(tk)
+        need(e, list(toks.items()))
+
+    def note(tk, r, w, add):
+        for k in r:
+            readers.setdefault(k, []).append(tk)
+        for k in w:
+            lastw[k], readers[k], epoch[k] = [tk], [], [tk]
+        for k in add:
+            lastw.setdefault(k, []).append(tk)
+
+    def op(e, f, r, w=(), add=()):
+        r, w, add = r.split(), (w.split() if w else []), (add.split() if add else [])
+        deps(e, r, w, add, True)
+        s = own[e]
+        f().then_inc(T.sem[s], 1)
+        tot[s] = tot.get(s, 0) + 1
+        note((s, tot[s]), r, w, add)
+
+    def dma(e, out, in_, s, r, w="", add=""):
+        r, w, add = r.split(), w.split(), add.split()
+        deps(e, r, w, add, False)
+        Q[e].dma_start(out, in_).then_inc(T.sem[s], 16)
+        tot[s] = tot.get(s, 0) + 16
+        note((s, None), r, w, add)
+
+    eng = topo.engines(core, mate)
+    ne = 1
+    while ne * 2 <= len(eng):
+        ne *= 2
+    msk = 0
+    for _e in eng[:ne]:
+        msk |= 1 << _e
+    rid, pid = topo.addr(mate)[:2]
+
+    def remote(out, in_, rs, ls, r, w):
+        deps("G", r.split(), [], [], False)
+        g.remote_dma(out_ap=out, in_ap=in_, remote_sem=T.sem[rs], local_sem=T.sem[ls], pid=pid, routing_id=rid, dma_engine_mask=msk)
+        tot[ls] = tot.get(ls, 0) + ne
+        tot[rs] = tot.get(rs, 0) + ne
+        note((ls, None), r.split(), [], [])
+        for k in w.split():
+            lastw.setdefault(k, []).append((rs, None))
+
+    v, ac, pe = g.vector, g.scalar, g.tensor
+
+    def ts(out, in0, s1, s2, o0, o1, r, w="", add=""):
+        if o1 is None:
+            op("V", lambda: v.tensor_scalar(out, in0, s1, None, o0), r, w, add)
+        else:
+            op("V", lambda: v.tensor_scalar(out, in0, s1, s2, o0, o1), r, w, add)
+
+    def tt(out, a, b, o, r, w="", add=""):
+        op("V", lambda: v.tensor_tensor(out, a, b, o), r, w, add)
+
+    def cp(out, a, r, w="", add=""):
+        op("V", lambda: v.tensor_copy(out, a), r, w, add)
+
+    def scan(out, d0, d1, ini, o0, o1, r, w="", add=""):
+        op("V", lambda: v.tensor_tensor_scan(out, d0, d1, ini, o0, o1), r, w, add)
+
+    def fill(ap, c, w="", add=""):
+        op("V", lambda: v.memset(ap, c), "", w, add)
+
+    def quant(c, s, t, r, w):
+        op("V", lambda: v.quantize_mx(c, s, t), r, w)
+
+    def act(out, in_, r, w="", add="", scale=1.0):
+        if scale == 1.0:
+            op("A", lambda: ac.activation(out, in_, AF.Copy), r, w, add)
+        else:
+            op("A", lambda: ac.activation(out, in_, AF.Copy, scale=scale), r, w, add)
+
+    def mm(out, l, ls, rr, rs, a, z, r, w="", add=""):
+        op("P", lambda: pe.matmul_mx(out, l, ls, rr, rs, a, z), r, w, add)
+
+    def iota(out, pat, base, ch, w, flag=True):
+        if flag:
+            op("G", lambda: g.iota(out, pat, base, ch, allow_small_or_imprecise_dtypes=True), "", w)
+        else:
+            op("G", lambda: g.iota(out, pat, base, ch), "", w)
+
+    dma("Y", T.X0[:], T.x[:], "dx", "", "X0")
+    dma("A", T.UT[:], T.u[:], "du", "", "UT")
+    dma("Y", T.WQ[:].bitcast(dt.uint8), T.wc[:], "dw", "", "WQ")
+    dma("Y", T.WS[:], T.ws[:], "dw", "", "WS")
+    dma("A", T.VT[:], T.v[:], "dv", "", "VT")
+
+    iota(T.IP[:, 0:1], [[0, 1]], 0, 1, "ip0", False)
+    iota(T.UI[:], [[3, 3], [0, 8]], 0, 1, "UI", False)
+    iota(T.I8[:], [[1, 16], [0, 8]], 0, 0, "I8")
+    iota(T.I16[:], [[0, 8], [1, 16]], 0, 0, "I16")
+    iota(T.JP[:, 0:128], [[4, 4], [1, 2], [16, 16]], 0, 0, "JP0")
+    iota(T.JP[:, 128:256], [[4, 4], [1, 2], [16, 16]], 2, 0, "JP1")
+    iota(T.ICOL[:], [[1, 512]], 0, 0, "ICOL")
+    iota(T.VB[:], [[1, 256]], 0, 0, "VB")
+    iota(T.PLF[:], [[-2, 2], [-4, 4], [-1, 2]], 255, 0, "PLF")
+    iota(T.IP[:, 8:10], [[128, 2]], 0, 1, "WI", False)
+    iota(T.JC[:, 16:32], [[2, 2], [0, 8]], 4352, 0, "JCF")
+    iota(T.JL[:, 16:32], [[16, 16]], 0, 0, "JLF")
+
+    for nm in ("CMT", "COT", "BT", "OT", "HMT"):
+        fill(T[nm][:], 0.0, nm)
+    IP, SC = T.IP, T.SC
+    for c, m in ((1, 15), (4, 1), (5, 3), (6, 7)):
+        ts(IP[:, c:c + 1], IP[:, 0:1], m, None, A.bitwise_and, None, "ip0", "ip%d" % c)
+    for c, m in ((2, 4), (3, 5)):
+        ts(IP[:, c:c + 1], IP[:, 0:1], m, None, A.arith_shift_right, None, "ip0", "ip%d" % c)
+
+    def sc(c):
+        return SC[:, c:c + 1]
+    for c, i, m, a in ((0, 0, 1.0, 0.0), (1, 1, 1.0, 0.0), (2, 2, 1.0, 0.0), (3, 2, 1.0, 8.0), (4, 0, 1.0, 128.0),
+                       (5, 0, -1.0, 255.0), (6, 0, -1.0, 127.0), (10, 1, 16.0, 0.0)):
+        ts(sc(c), IP[:, i:i + 1], m, a, A.mult, A.add, "ip%d" % i, "s%d" % c)
+    ts(T.UI[:], T.UI[:], 7, None, A.bitwise_and, None, "UI", "UI")
+    ts(T.UL[:], T.UI[:], 16, None, A.mult, None, "UI", "UL")
+    quant(T.UQ[:], T.US[:], T.UT[:], "UT", "UQ US")
+    cp(T.URQ[:].bitcast(dt.uint32), T.UQ[:].bitcast(dt.uint32).indirect(T.UL[:]), "UQ UL", "URQ")
+    op("A", lambda: ac.activation(T.URS[:], T.US[:].indirect(T.UL[:]), AF.Copy), "US UL", "URS")
+    ts(T.TH[:], T.I8[:], sc(1), 1e29, A.not_equal, A.mult, "I8 s1", "TH")
+    for h in range(2):
+        for b in range(2):
+            ts(T.CMT[:, 512 * h + b:512 * h + 512:4], T.I16[:], sc(2 + b), float(1 + h), A.is_equal, A.mult, "I16 s%d" % (2 + b), "", "CMT")
+    for s in range(2):
+        for b in range(2):
+            ts(T.COT[:, 512 * s + 2 + b:512 * s + 512:4], T.JP[:, 128 * s:128 * s + 128], sc(0 if b == 0 else 4), None, A.is_equal, None,
+               "JP%d s0 s4" % s, "", "COT")
+    quant(T.CMQ[:], T.CMS[:], T.CMT[:], "CMT", "CMQ CMS")
+    quant(T.COQ[:], T.COS[:], T.COT[:], "COT", "COQ COS")
+    fill(T.H50[:], 0.5, "H50")
+    fill(T.H50[:, 0::8], 0.0, "H50")
+
+    def setup_b():
+        for s in range(2):
+            for h in range(2):
+                ts(T.HMT[:, 1024 * h + s:1024 * h + 1024:4], T.ICOL[:, 0:256], sc(5 + s), 256.0, A.is_equal, A.mult, "ICOL s%d" % (5 + s), "", "HMT")
+        quant(T.HMQ[:], T.HMS[:], T.HMT[:], "HMT", "HMQ HMS")
+        fill(T.NEG[:], -1.0, "NEG")
+        ts(T.PL[:], T.PLF[:], sc(10), None, A.subtract, None, "PLF s10", "PL")
+        for b in range(4):
+            ts(T.MTT[:, b::4], T.ICOL[:, 0:256], sc(0 if b < 2 else 4), None, A.is_equal, None, "ICOL s0 s4", "", "MTT")
+        quant(T.MTQ[:], T.MTS[:], T.MTT[:], "MTT", "MTQ MTS")
+
+    so = [0]
+    for k in range(8):
+        so.append(so[-1] + 1 + (256 >> k))
+
+    def setup_c():
+        for k in range(8):
+            ts(T.NI[:, k:16:8], T.IP[:, 8:10], k, None, A.arith_shift_right, None, "WI", "", "NI")
+        fill(T.EQT[:], 1.0, "EQT")
+        fill(T.TB[:], 0.0, "ta0 ta1 tb0 tb1")
+        ts(T.NI[:, 16:32], T.NI[:, 0:16], 1, None, A.bitwise_and, None, "NI", "NB")
+        ts(T.NI[:, 32:48], T.NI[:, 16:32], -2, 1, A.mult, A.add, "NB", "NC")
+        tt(T.NS[:], T.NI[:, 0:16], T.NI[:, 32:48], A.add, "NI NC", "NS")
+        for h in range(2):
+            ts(T.TB[:, 784 * h:784 * h + 256], T.ICOL[:, 0:256], sc(4 * h), None, A.is_equal, None, "ICOL s%d" % (4 * h), "ta%d" % h)
+        for h in range(2):
+            for k in range(8):
+                o, n = 528 * h + so[k] + 1, 256 >> k
+                ts(T.EQT[:, o:o + n], T.ICOL[:, 0:n], T.NS[:, 8 * h + k:8 * h + k + 1], None, A.is_equal, None, "ICOL NS", "", "EQT")
+        for k in range(8):
+            for h in range(2):
+                o, n = 528 * h + so[k] + 1, 256 >> k
+                b = T.TB[:, 784 * h:784 * h + 256:1 << k]
+                tt(b, b, T.EQT[:, o:o + n], A.add, "EQT ta%d" % h, "ta%d" % h)
+        for h in range(2):
+            tt(T.TB[:, 784 * h + 257:784 * h + 774], T.EQT[:, 528 * h:528 * h + 517], T.EQT[:, 528 * h + 1:528 * h + 518], A.subtract, "EQT", "tb%d" % h)
+        for h in range(2):
+            a = T.TB[:, 784 * h:784 * h + 256]
+            ts(a, a, -256.0, None, A.mult, None, "ta%d" % h, "ta%d" % h)
+            a = T.TB[:, 784 * h + 257:784 * h + 774]
+            ts(a, a, 262144.0, None, A.mult, None, "tb%d" % h, "tb%d" % h)
+        for h in range(2):
+            dma("Y", T.tab[128 * h:128 * h + 128, :], T.TB[:, 784 * h:784 * h + 784], "dtab", "ta%d tb%d" % (h, h), "", "tab")
+
+    def setup_d():
+        fill(T.EHT[:], 0.0, "EHT")
+        fill(T.ELT[:], 0.0, "ELT")
+        for nm, c in (("EH", 0.5), ("EL", 32.0)):
+            for b in range(4):
+                ts(T[nm + "T"][:, 512 * b + b:512 * b + 512:4], T.ICOL[:, 0:128], sc(0), c, A.is_equal, A.mult, "ICOL s0", nm + "T")
+            quant(T[nm + "Q"][:], T[nm + "S"][:], T[nm + "T"][:], nm + "T", nm + "Q " + nm + "S")
+        for k in range(8):
+            fill(T.TK[:, k::8], 0.5 - 0.05 * 0.25 ** k, "", "TK")
+        fill(T.H25[:], 0.25, "H25")
+        fill(T.H25[:, 0::8], 0.0, "H25")
+        fill(T.H8[:], 1.0, "H8")
+        fill(T.H8[:, 0::8], 0.0, "H8")
+        fill(T.H10[:], 1.0, "H10")
+        fill(T.H10[:, 0::16], 0.0, "H10")
+        ts(sc(7), sc(10), sc(2), None, A.add, None, "s10 s2", "s7")
+        ts(sc(11), IP[:, 3:4], 2.0, None, A.mult, None, "ip3", "r0")
+        tt(sc(7), sc(7), sc(11), A.add, "s7 r0", "s7")
+        for i in range(3):
+            ts(sc(12 + i), IP[:, 4 + i:5 + i], 0.0, None, A.is_equal, None, "ip%d" % (4 + i), "r%d" % (1 + i))
+        tt(sc(8), sc(12), sc(13), A.add, "r1 r2", "s8")
+        tt(sc(8), sc(8), sc(14), A.add, "s8 r3", "s8")
+        ts(sc(9), IP[:, 1:2], 0.0, None, A.is_equal, None, "ip1", "s9")
+        for st, n in ((1, 2), (2, 4), (4, 8), (8, 16)):
+            fill(T.ILF[:, st:32:n], {1: 1.0, 2: 2.0, 4: 3.0, 8: 4.0}[st], "", "ILF")
+        fill(T.ILF[:, 0:1], 13.0, "", "ILF")
+        fill(T.ILF[:, 16:17], 6.0, "", "ILF")
+        ts(T.ILF[:, 32:64], T.ILF[:, 0:32], sc(9), sc(8), A.mult, A.add, "ILF s9 s8", "ILG")
+        cp(T.IL[:, 0:16], T.ILF[:, 32:48], "ILG", "IL0")
+        ts(T.IL[:, 16:32], T.ILF[:, 48:64], 8.0, None, A.add, None, "ILG", "IL1")
+        fill(T.AL[:], 0.0, "AL")
+        fill(T.YT[:], 0.0, "YT")
+        fill(T.DL[:], 0.0, "DL")
+        fill(T.AF[:], 0.0, "AF")
+        fill(T.ET[:, 384:512], 0.0, "ET4")
+        ts(T.JC[:, 0:16], T.JC[:, 16:32], sc(7), None, A.add, None, "JCF s7", "JC")
+        ts(T.JL[:, 0:16], T.JL[:, 16:32], sc(1), None, A.add, None, "JLF s1", "JL")
+        ts(T.MK[:], T.I16[:, 0:96], sc(1), None, A.is_equal, None, "I16 s1", "MK")
+
+    def B(b):
+        return T["B%d" % b]
+
+    DB = (2, 5, 6, 7)
+    for t in range(3):
+        last = t == 2
+        src, key = (T.X0, "X0") if t == 0 else (T.XT, "XT")
+        quant(T.XQ[:], T.XS[:], src[:], key, "XQ XS")
+        if t == 0:
+            for i in range(3):
+                dma("Y", T["AC%d" % i][:, 96:128].bitcast(dt.uint8), T.XQ[:, 0:32].bitcast(dt.uint8), "dfill", "XQ", "", "AC%d" % i)
+                dma("Y", T["AS%d" % i][:, 96:128], T.XS[:, 0:32], "dfill", "XS", "", "AS%d" % i)
+        for s in range(2):
+            mm(B(s)[:, 0:128], T.XQ[:, 128 * s:128 * s + 128], T.XS[:, 128 * s:128 * s + 128], T.URQ[:, 128 * t:128 * t + 128], T.URS[:, 128 * t:128 * t + 128],
+               True, True, "XQ XS URQ URS", "B%d" % s)
+        for s in range(2):
+            tt(T.BT[:, s:512:4], B(s)[:, 0:128], T.TH[:], A.is_gt, "B%d TH" % s, "", "BT")
+            ts(T.BT[:, 2 + s:512:4], B(s)[:, 0:128], 0.0, None, A.is_gt, None, "B%d" % s, "", "BT")
+        quant(T.BQ[:], T.BS[:], T.BT[:], "BT", "BQ BS")
+        mm(B(2)[:, 0:128], T.CMQ[:, 0:128], T.CMS[:, 0:128], T.BQ[:, 0:128], T.BS[:, 0:128], True, False, "CMQ CMS BQ BS", "B2")
+        mm(B(2)[:, 0:128], T.CMQ[:, 128:256], T.CMS[:, 128:256], T.BQ[:, 64:192], T.BS[:, 64:192], False, True, "CMQ CMS BQ BS", "", "B2")
+        for s in range(2):
+            mm(B(3 + s)[:, 0:128], T.COQ[:, 128 * s:128 * s + 128], T.COS[:, 128 * s:128 * s + 128], T.BQ[:, 0:128], T.BS[:, 0:128], True, True,
+               "COQ COS BQ BS", "B%d" % (3 + s))
+        act(T["MS%d" % t][:], B(2)[:, 0:64], "B2", "MS%d" % t)
+        remote(T["WL%d" % t][:], T["MS%d" % t][:], "wa%d" % t, "lw%d" % t, "MS%d" % t, "WL%d" % t)
+        for s in range(2):
+            ts(T.W8[:, 8 * s:8 * s + 8], B(s)[:, 0:8], 0.0, 128.0, A.is_gt, A.mult, "B%d" % s, "", "W8")
+        scan(T.W8[:, 16:32], T.H50[:], T.W8[:, 0:16], 0.0, A.mult, A.add, "H50 W8", "WW")
+        if t == 0:
+            setup_b()
+        for s in range(2):
+            ts(T.OT[:, s::4], T.VB[:], T.W8[:, 8 * s + 23:8 * s + 24], None, A.is_equal, None, "VB WW", "", "OT")
+        quant(T.OQ[:], T.OS[:], T.OT[:], "OT", "OQ OS")
+        for h in range(2):
+            mm(B(5 + h)[:], T.OQ[:, 128 * h:128 * h + 128], T.OS[:, 128 * h:128 * h + 128], T.HMQ[:], T.HMS[:], True, True, "OQ OS HMQ HMS", "B%d" % (5 + h))
+        for s in range(2):
+            ts(T.PB[:, 8 * s:8 * s + 8], B(3 + s)[:, 0:8], 128.0, None, A.mult, None, "B%d" % (3 + s), "", "PB")
+        scan(T.PB[:, 16:32], T.H50[:], T.PB[:, 0:16], 0.0, A.mult, A.add, "H50 PB", "PW")
+        cp(T.IX[:], T.PB[:, 23::8], "PW", "IX")
+        ts(T.SG[:, 0:16], T.PB[:, 0:16], -128.0, 8192.0, A.mult, A.add, "PB", "", "SG")
+        ts(T.SG[:, 16:32], T.PB[:, 0:16], -256.0, 16384.0, A.mult, A.add, "PB", "", "SG")
+        ts(T.SG[:, 32:48], T.PB[:, 0:16], 64.0, None, A.mult, None, "PB", "", "SG")
+        for h in range(2):
+            scan(T.DS[:, 512 * h:512 * h + 512], T.NEG[:], B(5 + h)[:], 0.0, A.add, A.max, "NEG B%d" % (5 + h), "DS%d" % h)
+        for h in range(2):
+            ts(T.DT[:, 2 * h::4], T.DS[:, 512 * h + 256:512 * h + 512].indirect(T.PL[:]), 201326592.0, 201326592.0, A.add, A.subtract,
+               "DS%d PL" % h, "", "DT")
+        for h in range(2):
+            for tk in lastw["DT"]:
+                need("V", [(tk[0], tot["cV"])])
+            tt(T.DT[:, 2 * h + 1::4], T.DS[:, 512 * h + 256:512 * h + 512].indirect(T.PL[:]), T.DT[:, 2 * h::4], A.subtract, "DS%d PL" % h, "", "DT")
+        quant(T.DQ[:], T.DP[:], T.DT[:], "DT", "DQ DP")
+        for s in range(2):
+            mm(B(s)[:, 0:256], T.DQ[:, 128 * s:128 * s + 128], T.DP[:, 128 * s:128 * s + 128], T.MTQ[:], T.MTS[:], True, True, "DQ DP MTQ MTS", "B%d" % s)
+        if t == 0:
+            setup_c()
+            setup_d()
+        deps("G", ["IX", "tab"], ["RS"], [], False)
+        for s in range(2):
+            g.indirect_dma_start(T.RS[:, 784 * s:784 * s + 784], None, T.tab[:], IndirectOffsetOnAxis(ap=T.IX[:, s:s + 1], axis=0),
+                                 bounds_check=255).then_inc(T.sem["di%d" % t], 16)
+        tot["di%d" % t] = 32
+        note(("di%d" % t, None), ["IX", "tab"], ["RS"], [])
+        for b in range(4):
+            mm(B(DB[b])[:, 0:256], T.EHQ[:, 128 * b:128 * b + 128], T.EHS[:, 128 * b:128 * b + 128], T.XQ[:], T.XS[:], True, True, "EHQ EHS XQ XS", "B%d" % DB[b])
+            act(T.HP[:, 256 * b:256 * b + 256], B(DB[b])[:, 0:256], "B%d" % DB[b], "", "HP")
+            act(T.HP[:, 1024 + 256 * b:1280 + 256 * b], B(DB[b])[:, 0:256], "B%d" % DB[b], "", "HP")
+        WL = T["WL%d" % t]
+        HI, HI2, LO, GS = T.HI[:, 0:64], T.HI[:, 64:128], T.HI[:, 128:192], T.GS[:, 0:32]
+        ts(HI2, WL[:], 2.0, 2.0, A.is_ge, A.mult, "WL%d" % t, "HI2")
+        ts(HI, WL[:], 2.0, None, A.is_ge, None, "WL%d" % t, "HI")
+        tt(LO, WL[:], HI2, A.subtract, "WL%d HI2" % t, "LO")
+        for s in range(2):
+            tt(T.E[:, 128 * s + 64:128 * s + 128], B(3 + s)[:, 64:128], HI, A.is_equal, "B%d HI" % (3 + s), "", "E")
+        for s in range(2):
+            tt(T.E[:, 128 * s:128 * s + 64], B(3 + s)[:, 0:64], LO, A.is_equal, "B%d LO" % (3 + s), "", "E")
+        scan(T.XH[:], T.H25[:], T.E[:], 0.0, A.mult, A.add, "H25 E", "XH")
+        GA = T.GS[:, 32:64]
+        ts(GA, T.XH[:, 7::8], -163840.0, 218445.0, A.mult, A.add, "XH", "GA")
+        op("V", lambda: v.reciprocal(GA, GA), "GA", "GA")
+        ts(GS, GA, 0.5, None, A.subtract, None, "GA", "GS")
+        for k in range(8):
+            for s in range(2):
+                c = 8 * s + k
+                op("V", lambda: v.tensor_reduce(T.RP[:, c:c + 1], T.GS[:, 16 * s:16 * s + 16], X, A.max, negate=True), "GS", "rp%d" % c)
+            if k == 7:
+                break
+            for s in range(2):
+                c = 8 * s + k
+                ts(T.TM[:, 16 * s:16 * s + 16], T.E[:, 128 * s + k:128 * s + 128:8], T.RP[:, c:c + 1], 0.062 * 0.25 ** k - 1.0, A.max, A.add,
+                   "E rp%d" % c, "tm%d" % s)
+            tt(GS, GS, T.TM[:], A.min, "GS tm0 tm1", "GS")
+        K = T.KK[:, 0:16]
+        tt(K, T.RP[:], T.TK[:], A.is_lt, "TK " + " ".join("rp%d" % c for c in range(16)), "K")
+        tt(T.KK[:, 16:32], K, T.SG[:, 0:16], A.mult, "K SG", "KA")
+        tt(T.KK[:, 32:48], K, T.SG[:, 16:32], A.mult, "K SG", "KB")
+        tt(T.KK[:, 48:64], K, T.SG[:, 32:48], A.mult, "K SG", "KC")
+        scan(T.KK[:, 80:96], T.H8[:], T.KK[:, 16:32], 0.0, A.mult, A.add, "H8 KA", "CU")
+        for s in range(2):
+            op("V", lambda: v.tensor_reduce(T.AL[:, 16 + s:17 + s], T.KK[:, 48 + 8 * s:56 + 8 * s], X, A.add), "KC AL", "al%d" % s)
+        tt(T.AL[:, 0:16], T.KK[:, 32:48], T.KK[:, 80:96], A.subtract, "KB CU AL", "al2")
+        for s in range(2):
+            tt(T.INC[:, 256 * s:256 * s + 256], T.AL[:].indirect(T.IL[:, 16 * s:16 * s + 16]), T.RS[:, 784 * s:784 * s + 256], A.add,
+               "al0 al1 al2 RS IL0 IL1", "INC%d" % s)
+        for s in range(2):
+            scan(T.O[:, 256 * s:256 * s + 256], T.INC[:, 256 * s:256 * s + 256], B(s)[:, 0:256], 0.0, A.add, A.max, "INC%d B%d" % (s, s), "O%d" % s)
+        for s in range(2):
+            for k in range(8):
+                n, e, o = 256 >> k, 256 * (8 * s + k + 1), 784 * s + 257 + so[k]
+                scan(T.XO[:, e - n:e], T.RS[:, o:o + n], T.O[:, 256 * s + (1 << k) - 1:256 * s + 256:1 << k], -65536.0, A.add, A.max, "RS O%d" % s, "", "XO")
+        K2 = T.KK[:, 64:80]
+        ts(K2, K, 256.0, None, A.mult, None, "K", "K2")
+        ts(T.YI[:, 0:16], T.XO[:, 255::256], 4096.0, None, A.add, None, "XO", "Y0")
+        ts(T.YI[:, 16:32], T.YI[:, 0:16], 8191, None, A.bitwise_and, None, "Y0", "Y1")
+        ts(T.YI[:, 32:48], T.YI[:, 16:32], 4096, None, A.max, None, "Y1", "Y2")
+        tt(T.YI[:, 48:64], T.JC[:, 0:16], T.YI[:, 32:48], A.subtract, "JC Y2", "YJ")
+        ts(T.YI[:, 0:16], T.YI[:, 48:64], 255, None, A.bitwise_and, None, "YJ", "Y0")
+        g0 = 3 * t % 8
+        for s in range(2):
+            for a, b, c in ((0, 8 - g0, g0), (8 - g0, 8, 0)):
+                if a < b:
+                    tt(T.YT[:, 16 * s + c:16 * s + c + b - a], T.YI[:, 8 * s + a:8 * s + b], T.KK[:, 64 + 8 * s + a:64 + 8 * s + b], A.add, "Y0 K2", "", "YT")
+        op("V", lambda: v.transpose(T.YT[:, 32:64], T.YT[:, 0:32]), "YT", "TR")
+        LB, lb = T["LB%d" % t], "LB%d" % t
+        for q in range(8):
+            dma("Y" if q % 2 == 0 else "A", LB[16 * q:16 * q + 16, :], T.YT[q::16, 32:64], "dl%d" % t, "TR", "", lb)
+        L = T.LF
+        ts(L[:, 0:16], LB[:], 256.0, 256.0, A.is_ge, A.mult, lb, "l0")
+        ts(T.DL[:, 0:16], LB[:], 256.0, None, A.is_lt, None, lb + " DL", "dl")
+        tt(T.AF[:, 0:16], LB[:], L[:, 0:16], A.subtract, lb + " l0 AF", "af")
+        op("V", lambda: v.transpose(T.DL[:, 32:64], T.DL[:, 0:32]), "dl", "dt")
+        cp(T.AU[:], T.AF[:, 0:16], "af", "AU")
+        scan(T.WC[:, 0:32], T.H10[:, 0:32], T.DL[:, 32:64], 0.0, A.mult, A.add, "H10 dt", "w0")
+
+        def mean(b):
+            tt(T.XW[:, 352 * b:352 * b + 256], T.HP[:, 256 * b:256 * b + 256].indirect(T.AU[:]), T.HP[:, 1024 + 256 * b:1280 + 256 * b], A.add, "HP AU", "XZ%d" % b)
+        mean(0)
+        for i in range(2):
+            ts(T.WC[:, 32 + 16 * i:48 + 16 * i], T.WC[:, 0:16], 0.0, T.WC[:, 16 * i + 15:16 * i + 16], A.mult, A.add, "w0", "w%d" % (1 + i))
+        op("V", lambda: v.transpose(T.WC[:, 64:128], T.WC[:, 0:64]), "w0 w1 w2", "wt")
+        ts(L[:, 16:32], T.DL[:, 0:16], -1024.0, None, A.mult, None, "dl", "l1")
+        JL = T.JL[:, 0:16]
+        tt(L[:, 32:48], L[:, 16:32], JL, A.add, "l1 JL", "l2")
+        Wi, Cn, Bi = T.WC[:, 64:80], T.WC[:, 96:112], T.WC[:, 128:144]
+        scan(Bi, T.NEG[:, 0:16], Cn, 0.0, A.max, A.add, "wt NEG", "bi")
+        mean(1)
+        tt(L[:, 48:64], Bi, Cn, A.subtract, "bi wt", "l3")
+        tt(L[:, 64:80], L[:, 48:64], Wi, A.add, "l3 wt", "l4")
+        ts(L[:, 80:96], L[:, 64:80], 1.0, None, A.subtract, None, "l4", "l5")
+        tt(L[:, 96:112], L[:, 32:48], L[:, 64:80], A.subtract, "l2 l4", "l6")
+        ts(L[:, 112:128], L[:, 96:112], T.WC[:, 143:144], None, A.add, None, "l6 bi", "l7")
+        tt(L[:, 128:144], L[:, 80:96], L[:, 112:128], A.max, "l5 l7", "pos")
+        cp(T.PU[:], L[:, 128:144], "pos", "PU")
+        mean(2)
+        op("V", lambda: v.tensor_copy(T.LR[:].indirect(T.PU[:]), T.ICOL[:, 0:256]), "PU ICOL", "LR")
+        tt(T.LM[:, 0:96], T.LR[:, 0:96], T.MK[:], A.mult, "LR MK", "lm")
+        scan(T.LM[:, 96:192], T.H10[:], T.LM[:, 0:96], 0.0, A.mult, A.add, "H10 lm", "ln")
+        cp(T.LU[:, 0:6], T.LM[:, 111::16], "ln", "LU")
+        mean(3)
+        for b in range(4):
+            o, i = T.ET[:, b:384:4], T.XW[:, 352 * b:352 * b + 256].indirect(T.LU[:, 0:6])
+            if b in (0, 2):
+                op("A", lambda: ac.activation(o, i, AF.Copy), "XZ%d LU" % b, "", "ET")
+            else:
+                op("V", lambda: v.tensor_copy(o, i), "XZ%d LU" % b, "", "ET")
+        quant(T.EQ[:], T.ES[:], T.ET[:], "ET ET4", "EQ ES")
+        remote(T["AC%d" % t][:, 0:96].bitcast(dt.uint8), T.EQ[:, 0:96].bitcast(dt.uint8), "ca%d" % t, "lc%d" % t, "EQ", "AC%d" % t)
+        remote(T["AS%d" % t][:, 0:96], T.ES[:, 0:96], "ca%d" % t, "lc%d" % t, "ES", "AS%d" % t)
+        ts(L[:, 144:160], L[:, 128:144], 96.0, None, A.is_lt, None, "pos", "m0")
+        tt(L[:, 160:176], L[:, 128:144], JL, A.subtract, "pos JL", "m1")
+        ts(L[:, 176:192], L[:, 160:176], 256.0, None, A.add, None, "m1", "m2")
+        tt(L[:, 160:176], L[:, 176:192], L[:, 144:160], A.mult, "m2 m0", "m3")
+        tt(L[:, 176:192], L[:, 160:176], JL, A.add, "m3 JL", "m2")
+        cp(T.SU[:], L[:, 176:192], "m2", "SU")
+        if last:
+            op("V", lambda: v.transpose(T.AF[:, 32:64], T.AF[:, 0:32]), "af", "at")
+            for q in range(8):
+                p = 32 * (q // 2)
+                dma("Y", T.al[q:q + 1, 0:256], T.AF[p:p + 16, 32 + 16 * (q % 2):48 + 16 * (q % 2)], "dout", "at")
+            dma("Y", T.al[:, 256:352], T.LR[0::16, 0:96], "dout", "LR")
+        AC, AS = T["AC%d" % t], T["AS%d" % t]
+        for b in range(4):
+            kb = "B%d" % DB[b]
+            mm(B(DB[b])[:, 0:128], T.WQ[:, 128 * b:128 * b + 128], T.WS[:, 128 * b:128 * b + 128], AC[:], AS[:], True, False, "WQ WS AC%d AS%d" % (t, t), kb)
+            mm(B(DB[b])[:, 0:128], T.ELQ[:, 128 * b:128 * b + 128], T.ELS[:, 128 * b:128 * b + 128], AC[:], AS[:], False, True, "ELQ ELS AC%d AS%d" % (t, t), "", kb)
+        for b in range(4):
+            kb, o, i = "B%d" % DB[b], T.XW[:, 352 * b + 256:352 * b + 352], B(DB[b])[:, 0:96]
+            if b % 2 == 0:
+                act(o, i, kb, "XT%d" % b, scale=0.03125)
+            else:
+                ts(o, i, 0.03125, None, A.mult, None, kb, "XT%d" % b)
+        for b in range(4):
+            o, i = T.XT[:, b::4], T.XW[:, 352 * b:352 * b + 352].indirect(T.SU[:])
+            if b % 2 == 0:
+                op("A", lambda: ac.activation(o, i, AF.Copy), "XZ%d XT%d SU" % (b, b), "", "XT")
+            else:
+                op("V", lambda: v.tensor_copy(o, i), "XZ%d XT%d SU" % (b, b), "", "XT")
+    quant(T.XQ[:], T.XS[:], T.XT[:], "XT", "XQ XS")
+    quant(T.VQ[:], T.VS[:], T.VT[:], "VT", "VQ VS")
+    dma("Y", T.oc[:], T.XQ[:].bitcast(dt.uint8), "dout", "XQ")
+    for k in range(4):
+        dma("A", T.osc[4 * k:4 * k + 4, :], T.XS[32 * k:32 * k + 4, :], "dout", "XS")
+    mm(B(3)[:, 0:256], T.VQ[:], T.VS[:], T.XQ[:], T.XS[:], True, True, "VQ VS XQ XS", "B3")
+    cp(T.YO[:], B(3)[:, 0:256], "B3", "YO")
+    dma("Y", T.y[:], T.YO[:], "dout", "YO")
+    for s in sorted(tot):
+        need("G", [(s, tot[s])])

@@ -6,16 +6,16 @@ SCRATCH = {}
 for _n, _w, _d in [
         ("X0", 1024, BF), ("UT", 512, BF), ("VT", 512, BF), ("WQ", 512, F8), ("WS", 512, U8),
         ("UQ", 128, F8), ("US", 128, U8), ("VQ", 128, F8), ("VS", 128, U8), ("URQ", 384, F8), ("URS", 384, U8),
-        ("EHT", 2048, BF), ("EHQ", 512, F8), ("EHS", 512, U8), ("ELT", 2048, BF), ("ELQ", 512, F8), ("ELS", 512, U8),
+        ("HT", 256, F32), ("ELT", 2048, BF), ("ELQ", 512, F8), ("ELS", 512, U8),
         ("CMT", 1024, BF), ("CMQ", 256, F8), ("CMS", 256, U8), ("COT", 1024, BF), ("COQ", 256, F8), ("COS", 256, U8),
         ("HMT", 2048, BF), ("HMQ", 512, F8), ("HMS", 512, U8), ("MTT", 1024, BF), ("MTQ", 256, F8), ("MTS", 256, U8),
-        ("ICOL", 512, F32), ("VB", 256, BF), ("I8", 128, F32), ("I16", 128, F32), ("JP", 256, F32), ("TH", 128, F32),
+        ("ICOL", 512, F32), ("VB", 256, BF), ("I8", 128, BF), ("I16", 128, BF), ("JP", 256, BF), ("TH", 128, F32),
         ("IP", 10, I32), ("SC", 16, F32), ("UI", 24, I32), ("UL", 24, U16), ("PLF", 16, F32), ("PL", 16, U16),
         ("ILF", 64, F32), ("IL", 32, U16), ("NI", 48, I32), ("NS", 16, F32),
-        ("EQT", 1056, BF), ("TB", 1568, BF), ("TK", 16, F32), ("H25", 256, BF), ("H50", 16, F32), ("H10", 96, F32),
-        ("H8", 16, F32), ("NEG", 512, F32), ("JC", 32, F32), ("JL", 32, F32), ("MK", 96, F32),
+        ("EQT", 1056, BF), ("TB", 1548, BF), ("TK", 16, F32), ("H25", 256, BF), ("H50", 16, F32), ("H10", 96, F32),
+        ("H8", 16, F32), ("NEG", 512, F32), ("JL", 32, F32), ("MK", 96, F32),
         ("XQ", 256, F8), ("XS", 256, U8), ("XT", 1024, BF), ("BT", 768, BF), ("BQ", 192, F8), ("BS", 192, U8),
-        ("W8", 32, F32), ("PB", 32, F32), ("IX", 2, I32), ("SG", 48, F32), ("RS", 1568, BF),
+        ("W8", 32, F32), ("PB", 32, F32), ("IX", 2, I32), ("SG", 48, F32), ("RS", 1548, BF),
         ("OT", 1024, BF), ("OQ", 256, F8), ("OS", 256, U8), ("DS", 1024, F32), ("DT", 1024, BF), ("DQ", 256, F8), ("DP", 256, U8),
         ("HI", 192, BF), ("E", 256, BF), ("XH", 256, F32), ("GS", 64, F32), ("TM", 32, F32),
         ("RP", 16, F32), ("KK", 96, F32), ("AL", 24, F32), ("INC", 512, F32), ("O", 512, F32), ("XO", 4096, F32),
@@ -34,7 +34,7 @@ for _t in range(3):
         SCRATCH["ES"] = ("sbuf", [128, 128], U8)
 for _b in range(8):
     SCRATCH["B%d" % _b] = ("psum", [128, 512], F32)
-SCRATCH["tab"] = ("dram", [256, 784], BF)
+SCRATCH["tab"] = ("dram", [256, 774], BF)
 SEMAPHORES = ["cV", "cA", "cP", "cG", "dx", "du", "dv", "dw", "dtab", "dfill", "dout"]
 for _t in range(3):
     SEMAPHORES += ["wa%d" % _t, "ca%d" % _t, "lw%d" % _t, "lc%d" % _t, "dl%d" % _t, "di%d" % _t]
@@ -173,19 +173,43 @@ def rank_program(g, core, T, topo):
 
     iota(T.IP[:, 0:1], [[0, 1]], 0, 1, "ip0", False)
     iota(T.UI[:], [[3, 3], [0, 8]], 0, 1, "UI", False)
+    iota(T.ICOL[:], [[1, 512]], 0, 0, "ICOL")
     iota(T.I8[:], [[1, 16], [0, 8]], 0, 0, "I8")
     iota(T.I16[:], [[0, 8], [1, 16]], 0, 0, "I16")
     iota(T.JP[:, 0:128], [[4, 4], [1, 2], [16, 16]], 0, 0, "JP0")
     iota(T.JP[:, 128:256], [[4, 4], [1, 2], [16, 16]], 2, 0, "JP1")
-    iota(T.ICOL[:], [[1, 512]], 0, 0, "ICOL")
     iota(T.VB[:], [[1, 256]], 0, 0, "VB")
     iota(T.PLF[:], [[-2, 2], [-4, 4], [-1, 2]], 255, 0, "PLF")
     iota(T.IP[:, 8:10], [[128, 2]], 0, 1, "WI", False)
-    iota(T.JC[:, 16:32], [[2, 2], [0, 8]], 4352, 0, "JCF")
     iota(T.JL[:, 16:32], [[16, 16]], 0, 0, "JLF")
+    iota(T.NEG[:], [[0, 512]], -1, 0, "NEG")
 
-    for nm in ("CMT", "COT", "BT", "OT", "HMT"):
+    DEAD = 262144.0
+
+    def flat(nm, width, c):
+        for a in range(0, width, 512):
+            b = min(width, a + 512)
+            o, i = T[nm][:, a:b], T.ICOL[:, 0:b - a]
+            if c == 0.0:
+                op("A", lambda: ac.activation(o, i, AF.Copy, scale=0.0), "ICOL", "", nm)
+            else:
+                op("A", lambda: ac.activation(o, i, AF.Identity, bias=c, scale=0.0), "ICOL", "", nm)
+        epoch[nm] = list(lastw[nm])
+
+    for k in range(8):
+        fill(T.TK[:, k::8], 0.5 - 0.05 * 0.25 ** k, "", "TK")
+    for nm, c, n in (("H50", 0.5, 8), ("H25", 0.25, 8), ("H8", 1.0, 8), ("H10", 1.0, 16)):
+        fill(T[nm][:], c, nm)
+        fill(T[nm][:, 0::n], 0.0, nm)
+    for st, n in ((1, 2), (2, 4), (4, 8), (8, 16)):
+        fill(T.ILF[:, st:32:n], {1: 1.0, 2: 2.0, 4: 3.0, 8: 4.0}[st], "", "ILF")
+    fill(T.ILF[:, 0:1], 13.0, "", "ILF")
+    fill(T.ILF[:, 16:17], 6.0, "", "ILF")
+    for nm in ("AL", "YT", "DL", "AF", "BT", "OT"):
         fill(T[nm][:], 0.0, nm)
+    fill(T.ET[:, 384:512], 0.0, "ET4")
+    flat("CMT", 1024, 0.0)
+    flat("COT", 1024, 0.0)
     IP, SC = T.IP, T.SC
     for c, m in ((1, 15), (4, 1), (5, 3), (6, 7)):
         ts(IP[:, c:c + 1], IP[:, 0:1], m, None, A.bitwise_and, None, "ip0", "ip%d" % c)
@@ -202,6 +226,8 @@ def rank_program(g, core, T, topo):
     quant(T.UQ[:], T.US[:], T.UT[:], "UT", "UQ US")
     cp(T.URQ[:].bitcast(dt.uint32), T.UQ[:].bitcast(dt.uint32).indirect(T.UL[:]), "UQ UL", "URQ")
     op("A", lambda: ac.activation(T.URS[:], T.US[:].indirect(T.UL[:]), AF.Copy), "US UL", "URS")
+    flat("EQT", 1056, DEAD)
+    flat("HMT", 2048, 0.0)
     ts(T.TH[:], T.I8[:], sc(1), 1e29, A.not_equal, A.mult, "I8 s1", "TH")
     for h in range(2):
         for b in range(2):
@@ -218,12 +244,11 @@ def rank_program(g, core, T, topo):
     def setup_b():
         for s in range(2):
             for h in range(2):
-                ts(T.HMT[:, 1024 * h + s:1024 * h + 1024:4], T.ICOL[:, 0:256], sc(5 + s), 256.0, A.is_equal, A.mult, "ICOL s%d" % (5 + s), "", "HMT")
+                ts(T.HMT[:, 1024 * h + s:1024 * h + 1024:4], T.VB[:], sc(5 + s), 256.0, A.is_equal, A.mult, "VB s%d" % (5 + s), "", "HMT")
         quant(T.HMQ[:], T.HMS[:], T.HMT[:], "HMT", "HMQ HMS")
-        fill(T.NEG[:], -1.0, "NEG")
         ts(T.PL[:], T.PLF[:], sc(10), None, A.subtract, None, "PLF s10", "PL")
         for b in range(4):
-            ts(T.MTT[:, b::4], T.ICOL[:, 0:256], sc(0 if b < 2 else 4), None, A.is_equal, None, "ICOL s0 s4", "", "MTT")
+            ts(T.MTT[:, b::4], T.VB[:], sc(0 if b < 2 else 4), None, A.is_equal, None, "VB s0 s4", "", "MTT")
         quant(T.MTQ[:], T.MTS[:], T.MTT[:], "MTT", "MTQ MTS")
 
     so = [0]
@@ -233,47 +258,37 @@ def rank_program(g, core, T, topo):
     def setup_c():
         for k in range(8):
             ts(T.NI[:, k:16:8], T.IP[:, 8:10], k, None, A.arith_shift_right, None, "WI", "", "NI")
-        fill(T.EQT[:], 1.0, "EQT")
-        fill(T.TB[:], 0.0, "ta0 ta1 tb0 tb1")
+        fill(T.TB[:, 773::774], 0.0, "tz")
         ts(T.NI[:, 16:32], T.NI[:, 0:16], 1, None, A.bitwise_and, None, "NI", "NB")
         ts(T.NI[:, 32:48], T.NI[:, 16:32], -2, 1, A.mult, A.add, "NB", "NC")
         tt(T.NS[:], T.NI[:, 0:16], T.NI[:, 32:48], A.add, "NI NC", "NS")
         for h in range(2):
-            ts(T.TB[:, 784 * h:784 * h + 256], T.ICOL[:, 0:256], sc(4 * h), None, A.is_equal, None, "ICOL s%d" % (4 * h), "ta%d" % h)
-        for h in range(2):
-            for k in range(8):
-                o, n = 528 * h + so[k] + 1, 256 >> k
-                ts(T.EQT[:, o:o + n], T.ICOL[:, 0:n], T.NS[:, 8 * h + k:8 * h + k + 1], None, A.is_equal, None, "ICOL NS", "", "EQT")
+            ts(T.TB[:, 774 * h:774 * h + 256], T.VB[:], sc(4 * h), DEAD, A.is_equal, A.mult, "VB s%d" % (4 * h), "ta%d" % h)
         for k in range(8):
             for h in range(2):
                 o, n = 528 * h + so[k] + 1, 256 >> k
-                b = T.TB[:, 784 * h:784 * h + 256:1 << k]
+                ts(T.EQT[:, o:o + n], T.VB[:, 0:n], T.NS[:, 8 * h + k:8 * h + k + 1], DEAD, A.is_equal, A.mult, "VB NS", "", "EQT")
+        for k in range(8):
+            for h in range(2):
+                o, n = 528 * h + so[k] + 1, 256 >> k
+                b = T.TB[:, 774 * h:774 * h + 256:1 << k]
                 tt(b, b, T.EQT[:, o:o + n], A.add, "EQT ta%d" % h, "ta%d" % h)
         for h in range(2):
-            tt(T.TB[:, 784 * h + 257:784 * h + 774], T.EQT[:, 528 * h:528 * h + 517], T.EQT[:, 528 * h + 1:528 * h + 518], A.subtract, "EQT", "tb%d" % h)
-        for h in range(2):
-            a = T.TB[:, 784 * h:784 * h + 256]
-            ts(a, a, -256.0, None, A.mult, None, "ta%d" % h, "ta%d" % h)
-            a = T.TB[:, 784 * h + 257:784 * h + 774]
-            ts(a, a, 262144.0, None, A.mult, None, "tb%d" % h, "tb%d" % h)
-        for h in range(2):
-            dma("Y", T.tab[128 * h:128 * h + 128, :], T.TB[:, 784 * h:784 * h + 784], "dtab", "ta%d tb%d" % (h, h), "", "tab")
+            a = T.TB[:, 774 * h:774 * h + 256]
+            ts(a, a, -256.0 / DEAD, None, A.mult, None, "ta%d" % h, "ta%d" % h)
+            tt(T.TB[:, 774 * h + 256:774 * h + 773], T.EQT[:, 528 * h:528 * h + 517], T.EQT[:, 528 * h + 1:528 * h + 518], A.subtract, "EQT", "tb%d" % h)
+            dma("Y", T.tab[128 * h:128 * h + 128, :], T.TB[:, 774 * h:774 * h + 774], "dtab", "ta%d tb%d tz" % (h, h), "", "tab")
+
+    def setup_e():
+        for b in range(4):
+            ts(T.ELT[:, 512 * b + b:512 * b + 512:4], T.VB[:, 0:128], sc(0), 32.0, A.is_equal, A.mult, "VB s0", "", "ELT")
+        quant(T.ELQ[:], T.ELS[:], T.ELT[:], "ELT", "ELQ ELS")
+
+    def setup_f():
+        ts(T.JL[:, 0:16], T.JL[:, 16:32], sc(1), None, A.add, None, "JLF s1", "JL")
+        ts(T.MK[:], T.I16[:, 0:96], sc(1), None, A.is_equal, None, "I16 s1", "MK")
 
     def setup_d():
-        fill(T.EHT[:], 0.0, "EHT")
-        fill(T.ELT[:], 0.0, "ELT")
-        for nm, c in (("EH", 0.5), ("EL", 32.0)):
-            for b in range(4):
-                ts(T[nm + "T"][:, 512 * b + b:512 * b + 512:4], T.ICOL[:, 0:128], sc(0), c, A.is_equal, A.mult, "ICOL s0", nm + "T")
-            quant(T[nm + "Q"][:], T[nm + "S"][:], T[nm + "T"][:], nm + "T", nm + "Q " + nm + "S")
-        for k in range(8):
-            fill(T.TK[:, k::8], 0.5 - 0.05 * 0.25 ** k, "", "TK")
-        fill(T.H25[:], 0.25, "H25")
-        fill(T.H25[:, 0::8], 0.0, "H25")
-        fill(T.H8[:], 1.0, "H8")
-        fill(T.H8[:, 0::8], 0.0, "H8")
-        fill(T.H10[:], 1.0, "H10")
-        fill(T.H10[:, 0::16], 0.0, "H10")
         ts(sc(7), sc(10), sc(2), None, A.add, None, "s10 s2", "s7")
         ts(sc(11), IP[:, 3:4], 2.0, None, A.mult, None, "ip3", "r0")
         tt(sc(7), sc(7), sc(11), A.add, "s7 r0", "s7")
@@ -282,21 +297,10 @@ def rank_program(g, core, T, topo):
         tt(sc(8), sc(12), sc(13), A.add, "r1 r2", "s8")
         tt(sc(8), sc(8), sc(14), A.add, "s8 r3", "s8")
         ts(sc(9), IP[:, 1:2], 0.0, None, A.is_equal, None, "ip1", "s9")
-        for st, n in ((1, 2), (2, 4), (4, 8), (8, 16)):
-            fill(T.ILF[:, st:32:n], {1: 1.0, 2: 2.0, 4: 3.0, 8: 4.0}[st], "", "ILF")
-        fill(T.ILF[:, 0:1], 13.0, "", "ILF")
-        fill(T.ILF[:, 16:17], 6.0, "", "ILF")
+        ts(sc(15), sc(7), 2.0, None, A.add, None, "s7", "s15")
         ts(T.ILF[:, 32:64], T.ILF[:, 0:32], sc(9), sc(8), A.mult, A.add, "ILF s9 s8", "ILG")
         cp(T.IL[:, 0:16], T.ILF[:, 32:48], "ILG", "IL0")
         ts(T.IL[:, 16:32], T.ILF[:, 48:64], 8.0, None, A.add, None, "ILG", "IL1")
-        fill(T.AL[:], 0.0, "AL")
-        fill(T.YT[:], 0.0, "YT")
-        fill(T.DL[:], 0.0, "DL")
-        fill(T.AF[:], 0.0, "AF")
-        fill(T.ET[:, 384:512], 0.0, "ET4")
-        ts(T.JC[:, 0:16], T.JC[:, 16:32], sc(7), None, A.add, None, "JCF s7", "JC")
-        ts(T.JL[:, 0:16], T.JL[:, 16:32], sc(1), None, A.add, None, "JLF s1", "JL")
-        ts(T.MK[:], T.I16[:, 0:96], sc(1), None, A.is_equal, None, "I16 s1", "MK")
 
     def B(b):
         return T["B%d" % b]
@@ -316,6 +320,8 @@ def rank_program(g, core, T, topo):
         for s in range(2):
             tt(T.BT[:, s:512:4], B(s)[:, 0:128], T.TH[:], A.is_gt, "B%d TH" % s, "", "BT")
             ts(T.BT[:, 2 + s:512:4], B(s)[:, 0:128], 0.0, None, A.is_gt, None, "B%d" % s, "", "BT")
+        for s in range(2):
+            ts(T.W8[:, 8 * s:8 * s + 8], B(s)[:, 0:8], 0.0, 128.0, A.is_gt, A.mult, "B%d" % s, "", "W8")
         quant(T.BQ[:], T.BS[:], T.BT[:], "BT", "BQ BS")
         mm(B(2)[:, 0:128], T.CMQ[:, 0:128], T.CMS[:, 0:128], T.BQ[:, 0:128], T.BS[:, 0:128], True, False, "CMQ CMS BQ BS", "B2")
         mm(B(2)[:, 0:128], T.CMQ[:, 128:256], T.CMS[:, 128:256], T.BQ[:, 64:192], T.BS[:, 64:192], False, True, "CMQ CMS BQ BS", "", "B2")
@@ -324,8 +330,17 @@ def rank_program(g, core, T, topo):
                "COQ COS BQ BS", "B%d" % (3 + s))
         act(T["MS%d" % t][:], B(2)[:, 0:64], "B2", "MS%d" % t)
         remote(T["WL%d" % t][:], T["MS%d" % t][:], "wa%d" % t, "lw%d" % t, "MS%d" % t, "WL%d" % t)
-        for s in range(2):
-            ts(T.W8[:, 8 * s:8 * s + 8], B(s)[:, 0:8], 0.0, 128.0, A.is_gt, A.mult, "B%d" % s, "", "W8")
+        def places():
+            for s in range(2):
+                ts(T.PB[:, 8 * s:8 * s + 8], B(3 + s)[:, 0:8], 128.0, None, A.mult, None, "B%d" % (3 + s), "", "PB")
+            scan(T.PB[:, 16:32], T.H50[:], T.PB[:, 0:16], 0.0, A.mult, A.add, "H50 PB", "PW")
+            ts(T.SG[:, 0:16], T.PB[:, 0:16], -128.0, 8192.0, A.mult, A.add, "PB", "", "SG")
+            cp(T.IX[:], T.PB[:, 23::8], "PW", "IX")
+            ts(T.SG[:, 16:32], T.PB[:, 0:16], -256.0, 16384.0, A.mult, A.add, "PB", "", "SG")
+            ts(T.SG[:, 32:48], T.PB[:, 0:16], 64.0, None, A.mult, None, "PB", "", "SG")
+        if t == 0:
+            places()
+            setup_c()
         scan(T.W8[:, 16:32], T.H50[:], T.W8[:, 0:16], 0.0, A.mult, A.add, "H50 W8", "WW")
         if t == 0:
             setup_b()
@@ -334,38 +349,37 @@ def rank_program(g, core, T, topo):
         quant(T.OQ[:], T.OS[:], T.OT[:], "OT", "OQ OS")
         for h in range(2):
             mm(B(5 + h)[:], T.OQ[:, 128 * h:128 * h + 128], T.OS[:, 128 * h:128 * h + 128], T.HMQ[:], T.HMS[:], True, True, "OQ OS HMQ HMS", "B%d" % (5 + h))
-        for s in range(2):
-            ts(T.PB[:, 8 * s:8 * s + 8], B(3 + s)[:, 0:8], 128.0, None, A.mult, None, "B%d" % (3 + s), "", "PB")
-        scan(T.PB[:, 16:32], T.H50[:], T.PB[:, 0:16], 0.0, A.mult, A.add, "H50 PB", "PW")
-        cp(T.IX[:], T.PB[:, 23::8], "PW", "IX")
-        ts(T.SG[:, 0:16], T.PB[:, 0:16], -128.0, 8192.0, A.mult, A.add, "PB", "", "SG")
-        ts(T.SG[:, 16:32], T.PB[:, 0:16], -256.0, 16384.0, A.mult, A.add, "PB", "", "SG")
-        ts(T.SG[:, 32:48], T.PB[:, 0:16], 64.0, None, A.mult, None, "PB", "", "SG")
+        if t == 0:
+            setup_d()
+        else:
+            places()
         for h in range(2):
             scan(T.DS[:, 512 * h:512 * h + 512], T.NEG[:], B(5 + h)[:], 0.0, A.add, A.max, "NEG B%d" % (5 + h), "DS%d" % h)
-        for h in range(2):
-            ts(T.DT[:, 2 * h::4], T.DS[:, 512 * h + 256:512 * h + 512].indirect(T.PL[:]), 201326592.0, 201326592.0, A.add, A.subtract,
-               "DS%d PL" % h, "", "DT")
-        for h in range(2):
-            for tk in lastw["DT"]:
-                need("V", [(tk[0], tot["cV"])])
-            tt(T.DT[:, 2 * h + 1::4], T.DS[:, 512 * h + 256:512 * h + 512].indirect(T.PL[:]), T.DT[:, 2 * h::4], A.subtract, "DS%d PL" % h, "", "DT")
-        quant(T.DQ[:], T.DP[:], T.DT[:], "DT", "DQ DP")
+        D0, D1 = [T.DS[:, 512 * h + 256:512 * h + 512].indirect(T.PL[:]) for h in range(2)]
+        op("A", lambda: ac.activation(T.HT[:], D0, AF.Identity, bias=201326592.0), "DS0 PL", "HT")
+        op("A", lambda: ac.activation(T.DT[:, 0::4], T.HT[:], AF.Identity, bias=-201326592.0), "HT", "dt0")
+        ts(T.DT[:, 2::4], D1, 201326592.0, 201326592.0, A.add, A.subtract, "DS1 PL", "dt2")
+        tt(T.DT[:, 1::4], D0, T.DT[:, 0::4], A.subtract, "DS0 PL dt0", "dt1")
+        tt(T.DT[:, 3::4], D1, T.DT[:, 2::4], A.subtract, "DS1 PL dt2", "dt3")
+        quant(T.DQ[:], T.DP[:], T.DT[:], "dt0 dt1 dt2 dt3", "DQ DP")
         for s in range(2):
             mm(B(s)[:, 0:256], T.DQ[:, 128 * s:128 * s + 128], T.DP[:, 128 * s:128 * s + 128], T.MTQ[:], T.MTS[:], True, True, "DQ DP MTQ MTS", "B%d" % s)
-        if t == 0:
-            setup_c()
-            setup_d()
         deps("G", ["IX", "tab"], ["RS"], [], False)
         for s in range(2):
-            g.indirect_dma_start(T.RS[:, 784 * s:784 * s + 784], None, T.tab[:], IndirectOffsetOnAxis(ap=T.IX[:, s:s + 1], axis=0),
+            g.indirect_dma_start(T.RS[:, 774 * s:774 * s + 774], None, T.tab[:], IndirectOffsetOnAxis(ap=T.IX[:, s:s + 1], axis=0),
                                  bounds_check=255).then_inc(T.sem["di%d" % t], 16)
         tot["di%d" % t] = 32
         note(("di%d" % t, None), ["IX", "tab"], ["RS"], [])
-        for b in range(4):
-            mm(B(DB[b])[:, 0:256], T.EHQ[:, 128 * b:128 * b + 128], T.EHS[:, 128 * b:128 * b + 128], T.XQ[:], T.XS[:], True, True, "EHQ EHS XQ XS", "B%d" % DB[b])
-            act(T.HP[:, 256 * b:256 * b + 256], B(DB[b])[:, 0:256], "B%d" % DB[b], "", "HP")
-            act(T.HP[:, 1024 + 256 * b:1280 + 256 * b], B(DB[b])[:, 0:256], "B%d" % DB[b], "", "HP")
+        def halves():
+            for b in range(4):
+                kb = "B%d" % DB[b]
+                mm(B(DB[b])[:, 0:256], T.ELQ[:, 128 * b:128 * b + 128], T.ELS[:, 128 * b:128 * b + 128], T.XQ[:], T.XS[:], True, True, "ELQ ELS XQ XS", kb)
+                for a in range(2):
+                    act(T.HP[:, 1024 * a + 256 * b:1024 * a + 256 * b + 256], B(DB[b])[:, 0:256], kb, "", "HP", scale=0.015625)
+        if t == 0:
+            flat("ELT", 2048, 0.0)
+        else:
+            halves()
         WL = T["WL%d" % t]
         HI, HI2, LO, GS = T.HI[:, 0:64], T.HI[:, 64:128], T.HI[:, 128:192], T.GS[:, 0:32]
         ts(HI2, WL[:], 2.0, 2.0, A.is_ge, A.mult, "WL%d" % t, "HI2")
@@ -380,17 +394,20 @@ def rank_program(g, core, T, topo):
         ts(GA, T.XH[:, 7::8], -163840.0, 218445.0, A.mult, A.add, "XH", "GA")
         op("V", lambda: v.reciprocal(GA, GA), "GA", "GA")
         ts(GS, GA, 0.5, None, A.subtract, None, "GA", "GS")
+        lastw["gs0"] = lastw["gs1"] = lastw["GS"]
         for k in range(8):
             for s in range(2):
                 c = 8 * s + k
-                op("V", lambda: v.tensor_reduce(T.RP[:, c:c + 1], T.GS[:, 16 * s:16 * s + 16], X, A.max, negate=True), "GS", "rp%d" % c)
+                op("V", lambda: v.tensor_reduce(T.RP[:, c:c + 1], T.GS[:, 16 * s:16 * s + 16], X, A.max, negate=True), "gs%d" % s, "rp%d" % c)
             if k == 7:
                 break
             for s in range(2):
                 c = 8 * s + k
                 ts(T.TM[:, 16 * s:16 * s + 16], T.E[:, 128 * s + k:128 * s + 128:8], T.RP[:, c:c + 1], 0.062 * 0.25 ** k - 1.0, A.max, A.add,
                    "E rp%d" % c, "tm%d" % s)
-            tt(GS, GS, T.TM[:], A.min, "GS tm0 tm1", "GS")
+            for s in range(2):
+                a = T.GS[:, 16 * s:16 * s + 16]
+                tt(a, a, T.TM[:, 16 * s:16 * s + 16], A.min, "gs%d tm%d" % (s, s), "gs%d" % s)
         K = T.KK[:, 0:16]
         tt(K, T.RP[:], T.TK[:], A.is_lt, "TK " + " ".join("rp%d" % c for c in range(16)), "K")
         tt(T.KK[:, 16:32], K, T.SG[:, 0:16], A.mult, "K SG", "KA")
@@ -400,21 +417,24 @@ def rank_program(g, core, T, topo):
         for s in range(2):
             op("V", lambda: v.tensor_reduce(T.AL[:, 16 + s:17 + s], T.KK[:, 48 + 8 * s:56 + 8 * s], X, A.add), "KC AL", "al%d" % s)
         tt(T.AL[:, 0:16], T.KK[:, 32:48], T.KK[:, 80:96], A.subtract, "KB CU AL", "al2")
+        if t == 0:
+            setup_e()
+            halves()
         for s in range(2):
-            tt(T.INC[:, 256 * s:256 * s + 256], T.AL[:].indirect(T.IL[:, 16 * s:16 * s + 16]), T.RS[:, 784 * s:784 * s + 256], A.add,
+            tt(T.INC[:, 256 * s:256 * s + 256], T.AL[:].indirect(T.IL[:, 16 * s:16 * s + 16]), T.RS[:, 774 * s:774 * s + 256], A.add,
                "al0 al1 al2 RS IL0 IL1", "INC%d" % s)
         for s in range(2):
             scan(T.O[:, 256 * s:256 * s + 256], T.INC[:, 256 * s:256 * s + 256], B(s)[:, 0:256], 0.0, A.add, A.max, "INC%d B%d" % (s, s), "O%d" % s)
         for s in range(2):
             for k in range(8):
-                n, e, o = 256 >> k, 256 * (8 * s + k + 1), 784 * s + 257 + so[k]
+                n, e, o = 256 >> k, 256 * (8 * s + k + 1), 774 * s + 256 + so[k]
                 scan(T.XO[:, e - n:e], T.RS[:, o:o + n], T.O[:, 256 * s + (1 << k) - 1:256 * s + 256:1 << k], -65536.0, A.add, A.max, "RS O%d" % s, "", "XO")
         K2 = T.KK[:, 64:80]
         ts(K2, K, 256.0, None, A.mult, None, "K", "K2")
-        ts(T.YI[:, 0:16], T.XO[:, 255::256], 4096.0, None, A.add, None, "XO", "Y0")
+        ts(T.YI[:, 0:16], T.XO[:, 255::256], -1.0, 4096.0, A.mult, A.add, "XO", "Y0")
         ts(T.YI[:, 16:32], T.YI[:, 0:16], 8191, None, A.bitwise_and, None, "Y0", "Y1")
-        ts(T.YI[:, 32:48], T.YI[:, 16:32], 4096, None, A.max, None, "Y1", "Y2")
-        tt(T.YI[:, 48:64], T.JC[:, 0:16], T.YI[:, 32:48], A.subtract, "JC Y2", "YJ")
+        for s in range(2):
+            ts(T.YI[:, 48 + 8 * s:56 + 8 * s], T.YI[:, 16 + 8 * s:24 + 8 * s], 4096.0, sc(7 + 8 * s), A.min, A.add, "Y1 s7 s15", "", "YJ")
         ts(T.YI[:, 0:16], T.YI[:, 48:64], 255, None, A.bitwise_and, None, "YJ", "Y0")
         g0 = 3 * t % 8
         for s in range(2):
@@ -425,6 +445,8 @@ def rank_program(g, core, T, topo):
         LB, lb = T["LB%d" % t], "LB%d" % t
         for q in range(8):
             dma("Y" if q % 2 == 0 else "A", LB[16 * q:16 * q + 16, :], T.YT[q::16, 32:64], "dl%d" % t, "TR", "", lb)
+        if t == 0:
+            setup_f()
         L = T.LF
         ts(L[:, 0:16], LB[:], 256.0, 256.0, A.is_ge, A.mult, lb, "l0")
         ts(T.DL[:, 0:16], LB[:], 256.0, None, A.is_lt, None, lb + " DL", "dl")

@@ -8,25 +8,25 @@ for _n, _w, _d in [
         ("UQ", 128, F8), ("US", 128, U8), ("VQ", 128, F8), ("VS", 128, U8), ("URQ", 384, F8), ("URS", 384, U8),
         ("HT", 256, F32), ("ELT", 2048, BF), ("ELQ", 512, F8), ("ELS", 512, U8),
         ("CMT", 1024, BF), ("CMQ", 256, F8), ("CMS", 256, U8), ("COT", 1024, BF), ("COQ", 256, F8), ("COS", 256, U8),
-        ("HMT", 2048, BF), ("HMQ", 512, F8), ("HMS", 512, U8), ("MTT", 1024, BF), ("MTQ", 256, F8), ("MTS", 256, U8),
+        ("HMT", 1024, BF), ("HMQ", 256, F8), ("HMS", 256, U8), ("MTT", 1024, BF), ("MTQ", 256, F8), ("MTS", 256, U8),
         ("ICOL", 512, F32), ("VB", 256, BF), ("I8", 128, BF), ("I16", 128, BF), ("JP", 256, BF), ("TH", 128, F32),
         ("IP", 10, I32), ("SC", 16, F32), ("UI", 24, I32), ("UL", 24, U16), ("PLF", 16, F32), ("PL", 16, U16),
         ("ILF", 64, F32), ("IL", 32, U16), ("NI", 48, I32), ("NS", 16, F32),
-        ("EQT", 1056, BF), ("TB", 1548, BF), ("TK", 16, F32), ("H25", 256, BF), ("H50", 16, F32), ("H10", 96, F32),
-        ("H8", 16, F32), ("NEG", 512, F32), ("JL", 32, F32), ("MK", 96, F32),
+        ("EQT", 518, BF), ("TB", 1548, BF), ("TK", 16, F32), ("H25", 256, BF), ("H50", 16, F32), ("H10", 96, F32),
+        ("H8", 16, F32), ("NEG", 256, F32), ("JL", 32, F32), ("MK", 192, F32),
         ("XQ", 256, F8), ("XS", 256, U8), ("XT", 1024, BF), ("BT", 768, BF), ("BQ", 192, F8), ("BS", 192, U8),
         ("W8", 32, F32), ("PB", 32, F32), ("IX", 2, I32), ("SG", 48, F32), ("RS", 1548, BF),
         ("OT", 1024, BF), ("OQ", 256, F8), ("OS", 256, U8), ("DS", 1024, F32), ("DT", 1024, BF), ("DQ", 256, F8), ("DP", 256, U8),
         ("HI", 192, BF), ("E", 256, BF), ("XH", 256, F32), ("GS", 64, F32), ("TM", 32, F32),
         ("RP", 16, F32), ("KK", 96, F32), ("AL", 24, F32), ("INC", 512, F32), ("O", 512, F32), ("XO", 4096, F32),
-        ("YI", 64, I32), ("YT", 64, F32),
+        ("YI", 64, I32), ("YT", 64, I32), ("AI", 16, I32),
         ("LF", 192, F32), ("DL", 64, F32), ("AF", 64, F32), ("WC", 160, F32), ("AU", 16, U16), ("PU", 16, U16), ("LU", 8, U16), ("SU", 16, U16),
-        ("LR", 256, F32), ("LM", 192, F32), ("HP", 2048, BF), ("XW", 1408, BF), ("ET", 512, BF), ("YO", 256, F32)]:
+        ("LR", 256, F32), ("LM", 96, F32), ("HP", 2048, BF), ("XW", 1408, BF), ("ET", 512, BF), ("YO", 256, F32)]:
     SCRATCH[_n] = ("sbuf", [128, _w], _d)
 for _t in range(3):
     SCRATCH["MS%d" % _t] = ("sbuf", [128, 64], BF)
     SCRATCH["WL%d" % _t] = ("sbuf", [128, 64], BF)
-    SCRATCH["LB%d" % _t] = ("sbuf", [128, 16], F32)
+    SCRATCH["LB%d" % _t] = ("sbuf", [128, 16], I32)
     SCRATCH["AC%d" % _t] = ("sbuf", [128, 128], F8)
     SCRATCH["AS%d" % _t] = ("sbuf", [128, 128], U8)
     if _t == 0:
@@ -182,7 +182,7 @@ def rank_program(g, core, T, topo):
     iota(T.PLF[:], [[-2, 2], [-4, 4], [-1, 2]], 255, 0, "PLF")
     iota(T.IP[:, 8:10], [[128, 2]], 0, 1, "WI", False)
     iota(T.JL[:, 16:32], [[16, 16]], 0, 0, "JLF")
-    iota(T.NEG[:], [[0, 512]], -1, 0, "NEG")
+    iota(T.NEG[:], [[0, 256]], -1, 0, "NEG")
 
     DEAD = 262144.0
 
@@ -197,7 +197,7 @@ def rank_program(g, core, T, topo):
         epoch[nm] = list(lastw[nm])
 
     for k in range(8):
-        fill(T.TK[:, k::8], 0.5 - 0.05 * 0.25 ** k, "", "TK")
+        fill(T.TK[:, k::8], 0.05 * 0.25 ** k, "", "TK")
     for nm, c, n in (("H50", 0.5, 8), ("H25", 0.25, 8), ("H8", 1.0, 8), ("H10", 1.0, 16)):
         fill(T[nm][:], c, nm)
         fill(T[nm][:, 0::n], 0.0, nm)
@@ -205,7 +205,8 @@ def rank_program(g, core, T, topo):
         fill(T.ILF[:, st:32:n], {1: 1.0, 2: 2.0, 4: 3.0, 8: 4.0}[st], "", "ILF")
     fill(T.ILF[:, 0:1], 13.0, "", "ILF")
     fill(T.ILF[:, 16:17], 6.0, "", "ILF")
-    for nm in ("AL", "YT", "DL", "AF", "BT", "OT"):
+    fill(T.YT[:], 0, "YT")
+    for nm in ("AL", "DL", "AF", "BT", "OT"):
         fill(T[nm][:], 0.0, nm)
     fill(T.ET[:, 384:512], 0.0, "ET4")
     flat("CMT", 1024, 0.0)
@@ -226,8 +227,24 @@ def rank_program(g, core, T, topo):
     quant(T.UQ[:], T.US[:], T.UT[:], "UT", "UQ US")
     cp(T.URQ[:].bitcast(dt.uint32), T.UQ[:].bitcast(dt.uint32).indirect(T.UL[:]), "UQ UL", "URQ")
     op("A", lambda: ac.activation(T.URS[:], T.US[:].indirect(T.UL[:]), AF.Copy), "US UL", "URS")
-    flat("EQT", 1056, DEAD)
-    flat("HMT", 2048, 0.0)
+    so = [0]
+    for k in range(8):
+        so.append(so[-1] + 1 + (256 >> k))
+
+    def ones(nm, o, n, c):
+        op("A", lambda: ac.activation(T[nm][:, o:o + n], T.ICOL[:, 0:n], AF.Identity, bias=c, scale=0.0), "ICOL", "", nm)
+    flat("EQT", 518, 0.0)
+    for k in range(8):
+        ones("EQT", so[k], 1, DEAD)
+    ones("EQT", so[7] + 2, 1, DEAD)
+    epoch["EQT"] = list(lastw["EQT"])
+    for o, n, c in ((129, 127, 0.0), (773, 1, 0.0), (775, 127, 0.0), (1030, 512, 0.0), (1542, 6, 0.0), (128, 1, -256.0), (774, 1, -256.0)):
+        ones("TB", o, n, c)
+    epoch["TB"] = list(lastw["TB"])
+    for k in range(8):
+        ones("TB", 1030 + so[k] + (1 if k == 7 else 0), 1, DEAD)
+    epoch["tb1"] = list(lastw["TB"])
+    flat("HMT", 1024, 0.0)
     ts(T.TH[:], T.I8[:], sc(1), 1e29, A.not_equal, A.mult, "I8 s1", "TH")
     for h in range(2):
         for b in range(2):
@@ -243,41 +260,40 @@ def rank_program(g, core, T, topo):
 
     def setup_b():
         for s in range(2):
-            for h in range(2):
-                ts(T.HMT[:, 1024 * h + s:1024 * h + 1024:4], T.VB[:], sc(5 + s), 256.0, A.is_equal, A.mult, "VB s%d" % (5 + s), "", "HMT")
+            if True:
+                ts(T.HMT[:, s::4], T.VB[:], sc(5 + s), 256.0, A.is_equal, A.mult, "VB s%d" % (5 + s), "", "HMT")
         quant(T.HMQ[:], T.HMS[:], T.HMT[:], "HMT", "HMQ HMS")
         ts(T.PL[:], T.PLF[:], sc(10), None, A.subtract, None, "PLF s10", "PL")
         for b in range(4):
             ts(T.MTT[:, b::4], T.VB[:], sc(0 if b < 2 else 4), None, A.is_equal, None, "VB s0 s4", "", "MTT")
         quant(T.MTQ[:], T.MTS[:], T.MTT[:], "MTT", "MTQ MTS")
 
-    so = [0]
-    for k in range(8):
-        so.append(so[-1] + 1 + (256 >> k))
-
     def setup_c():
         for k in range(8):
             ts(T.NI[:, k:16:8], T.IP[:, 8:10], k, None, A.arith_shift_right, None, "WI", "", "NI")
-        fill(T.TB[:, 773::774], 0.0, "tz")
         ts(T.NI[:, 16:32], T.NI[:, 0:16], 1, None, A.bitwise_and, None, "NI", "NB")
         ts(T.NI[:, 32:48], T.NI[:, 16:32], -2, 1, A.mult, A.add, "NB", "NC")
         tt(T.NS[:], T.NI[:, 0:16], T.NI[:, 32:48], A.add, "NI NC", "NS")
+        a = T.TB[:, 0:128]
+        ts(a, T.VB[:, 0:128], sc(0), DEAD, A.is_equal, A.mult, "VB s0", "ta0")
+        for k in range(7):
+            o, n = so[k] + 1, 128 >> k
+            ts(T.EQT[:, o:o + n], T.VB[:, 0:n], T.NS[:, k:k + 1], DEAD, A.is_equal, A.mult, "VB NS", "", "EQT")
+        tt(T.TB[:, 256:773], T.EQT[:, 0:517], T.EQT[:, 1:518], A.subtract, "EQT", "tb0")
+        for k in range(7):
+            o, n = 256 + so[k], 128 >> k
+            i1, o1, i2, o2 = T.TB[:, o + 1:o + n], T.TB[:, 774 + o + n + 1:774 + o + 2 * n], T.TB[:, o:o + 1], T.TB[:, 774 + o + n:774 + o + n + 1]
+            if n > 1:
+                act(o1, i1, "tb0 TB", "", "tb1")
+            op("A", lambda: ac.activation(o2, i2, AF.Identity, bias=-DEAD, scale=1.0), "tb0 TB", "", "tb1")
+        for k in range(7):
+            o, n = so[k] + 1, 128 >> k
+            b = T.TB[:, 0:128:1 << k]
+            tt(b, b, T.EQT[:, o:o + n], A.add, "EQT ta0", "ta0")
+        ts(a, a, -256.0 / DEAD, None, A.mult, None, "ta0", "ta0")
+        act(T.TB[:, 902:1030], a, "ta0", "ta1")
         for h in range(2):
-            ts(T.TB[:, 774 * h:774 * h + 256], T.VB[:], sc(4 * h), DEAD, A.is_equal, A.mult, "VB s%d" % (4 * h), "ta%d" % h)
-        for k in range(8):
-            for h in range(2):
-                o, n = 528 * h + so[k] + 1, 256 >> k
-                ts(T.EQT[:, o:o + n], T.VB[:, 0:n], T.NS[:, 8 * h + k:8 * h + k + 1], DEAD, A.is_equal, A.mult, "VB NS", "", "EQT")
-        for k in range(8):
-            for h in range(2):
-                o, n = 528 * h + so[k] + 1, 256 >> k
-                b = T.TB[:, 774 * h:774 * h + 256:1 << k]
-                tt(b, b, T.EQT[:, o:o + n], A.add, "EQT ta%d" % h, "ta%d" % h)
-        for h in range(2):
-            a = T.TB[:, 774 * h:774 * h + 256]
-            ts(a, a, -256.0 / DEAD, None, A.mult, None, "ta%d" % h, "ta%d" % h)
-            tt(T.TB[:, 774 * h + 256:774 * h + 773], T.EQT[:, 528 * h:528 * h + 517], T.EQT[:, 528 * h + 1:528 * h + 518], A.subtract, "EQT", "tb%d" % h)
-            dma("Y", T.tab[128 * h:128 * h + 128, :], T.TB[:, 774 * h:774 * h + 774], "dtab", "ta%d tb%d tz" % (h, h), "", "tab")
+            dma("Y", T.tab[128 * h:128 * h + 128, :], T.TB[:, 774 * h:774 * h + 774], "dtab", "ta%d tb%d TB" % (h, h), "", "tab")
 
     def setup_e():
         for b in range(4):
@@ -286,7 +302,11 @@ def rank_program(g, core, T, topo):
 
     def setup_f():
         ts(T.JL[:, 0:16], T.JL[:, 16:32], sc(1), None, A.add, None, "JLF s1", "JL")
-        ts(T.MK[:], T.I16[:, 0:96], sc(1), None, A.is_equal, None, "I16 s1", "MK")
+        ts(T.MK[:, 96:192], T.I16[:, 0:96], sc(1), 8000.0, A.not_equal, A.mult, "I16 s1", "mk0")
+        tt(T.MK[:, 1:96], T.MK[:, 97:192], T.MK[:, 96:191], A.subtract, "mk0", "MK")
+        ts(T.MK[:, 16:96:16], T.MK[:, 16:96:16], 3000.0, None, A.subtract, None, "MK", "MK")
+        cp(T.MK[:, 0:1], T.MK[:, 96:97], "mk0 MK", "MK")
+        quant(T.VQ[:], T.VS[:], T.VT[:], "VT", "VQ VS")
 
     def setup_d():
         ts(sc(7), sc(10), sc(2), None, A.add, None, "s10 s2", "s7")
@@ -309,14 +329,15 @@ def rank_program(g, core, T, topo):
     for t in range(3):
         last = t == 2
         src, key = (T.X0, "X0") if t == 0 else (T.XT, "XT")
-        quant(T.XQ[:], T.XS[:], src[:], key, "XQ XS")
+        for h in range(2):
+            quant(T.XQ[:, 128 * h:128 * h + 128], T.XS[:, 128 * h:128 * h + 128], src[:, 512 * h:512 * h + 512], key, "XQ%d" % h)
         if t == 0:
             for i in range(3):
-                dma("Y", T["AC%d" % i][:, 96:128].bitcast(dt.uint8), T.XQ[:, 0:32].bitcast(dt.uint8), "dfill", "XQ", "", "AC%d" % i)
-                dma("Y", T["AS%d" % i][:, 96:128], T.XS[:, 0:32], "dfill", "XS", "", "AS%d" % i)
+                dma("Y", T["AC%d" % i][:, 96:128].bitcast(dt.uint8), T.XQ[:, 0:32].bitcast(dt.uint8), "dfill", "XQ0", "", "AC%d" % i)
+                dma("Y", T["AS%d" % i][:, 96:128], T.XS[:, 0:32], "dfill", "XQ0", "", "AS%d" % i)
         for s in range(2):
             mm(B(s)[:, 0:128], T.XQ[:, 128 * s:128 * s + 128], T.XS[:, 128 * s:128 * s + 128], T.URQ[:, 128 * t:128 * t + 128], T.URS[:, 128 * t:128 * t + 128],
-               True, True, "XQ XS URQ URS", "B%d" % s)
+               True, True, "XQ%d URQ URS" % s, "B%d" % s)
         for s in range(2):
             tt(T.BT[:, s:512:4], B(s)[:, 0:128], T.TH[:], A.is_gt, "B%d TH" % s, "", "BT")
             ts(T.BT[:, 2 + s:512:4], B(s)[:, 0:128], 0.0, None, A.is_gt, None, "B%d" % s, "", "BT")
@@ -348,13 +369,16 @@ def rank_program(g, core, T, topo):
             ts(T.OT[:, s::4], T.VB[:], T.W8[:, 8 * s + 23:8 * s + 24], None, A.is_equal, None, "VB WW", "", "OT")
         quant(T.OQ[:], T.OS[:], T.OT[:], "OT", "OQ OS")
         for h in range(2):
-            mm(B(5 + h)[:], T.OQ[:, 128 * h:128 * h + 128], T.OS[:, 128 * h:128 * h + 128], T.HMQ[:], T.HMS[:], True, True, "OQ OS HMQ HMS", "B%d" % (5 + h))
+            mm(B(5 + h)[:, 0:256], T.OQ[:, 128 * h:128 * h + 128], T.OS[:, 128 * h:128 * h + 128], T.HMQ[:], T.HMS[:], True, True, "OQ OS HMQ HMS", "B%d" % (5 + h))
         if t == 0:
             setup_d()
         else:
             places()
         for h in range(2):
-            scan(T.DS[:, 512 * h:512 * h + 512], T.NEG[:], B(5 + h)[:], 0.0, A.add, A.max, "NEG B%d" % (5 + h), "DS%d" % h)
+            scan(T.DS[:, 512 * h:512 * h + 256], T.NEG[:], B(5 + h)[:, 0:256], 0.0, A.add, A.max, "NEG B%d" % (5 + h), "DR%d" % h)
+        for h in range(2):
+            scan(T.DS[:, 512 * h + 256:512 * h + 512], T.NEG[:], B(5 + h)[:, 0:256], T.DS[:, 512 * h + 255:512 * h + 256], A.add, A.max,
+                 "NEG DR%d B%d" % (h, 5 + h), "DS%d" % h)
         D0, D1 = [T.DS[:, 512 * h + 256:512 * h + 512].indirect(T.PL[:]) for h in range(2)]
         op("A", lambda: ac.activation(T.HT[:], D0, AF.Identity, bias=201326592.0), "DS0 PL", "HT")
         op("A", lambda: ac.activation(T.DT[:, 0::4], T.HT[:], AF.Identity, bias=-201326592.0), "HT", "dt0")
@@ -373,7 +397,7 @@ def rank_program(g, core, T, topo):
         def halves():
             for b in range(4):
                 kb = "B%d" % DB[b]
-                mm(B(DB[b])[:, 0:256], T.ELQ[:, 128 * b:128 * b + 128], T.ELS[:, 128 * b:128 * b + 128], T.XQ[:], T.XS[:], True, True, "ELQ ELS XQ XS", kb)
+                mm(B(DB[b])[:, 0:256], T.ELQ[:, 128 * b:128 * b + 128], T.ELS[:, 128 * b:128 * b + 128], T.XQ[:], T.XS[:], True, True, "ELQ ELS XQ0 XQ1", kb)
                 for a in range(2):
                     act(T.HP[:, 1024 * a + 256 * b:1024 * a + 256 * b + 256], B(DB[b])[:, 0:256], kb, "", "HP", scale=0.015625)
         if t == 0:
@@ -386,30 +410,29 @@ def rank_program(g, core, T, topo):
         ts(HI, WL[:], 2.0, None, A.is_ge, None, "WL%d" % t, "HI")
         tt(LO, WL[:], HI2, A.subtract, "WL%d HI2" % t, "LO")
         for s in range(2):
-            tt(T.E[:, 128 * s + 64:128 * s + 128], B(3 + s)[:, 64:128], HI, A.is_equal, "B%d HI" % (3 + s), "", "E")
+            tt(T.E[:, 128 * s + 64:128 * s + 128], B(3 + s)[:, 64:128], HI, A.not_equal, "B%d HI" % (3 + s), "", "E")
         for s in range(2):
-            tt(T.E[:, 128 * s:128 * s + 64], B(3 + s)[:, 0:64], LO, A.is_equal, "B%d LO" % (3 + s), "", "E")
+            tt(T.E[:, 128 * s:128 * s + 64], B(3 + s)[:, 0:64], LO, A.not_equal, "B%d LO" % (3 + s), "", "E")
         scan(T.XH[:], T.H25[:], T.E[:], 0.0, A.mult, A.add, "H25 E", "XH")
         GA = T.GS[:, 32:64]
-        ts(GA, T.XH[:, 7::8], -163840.0, 218445.0, A.mult, A.add, "XH", "GA")
-        op("V", lambda: v.reciprocal(GA, GA), "GA", "GA")
-        ts(GS, GA, 0.5, None, A.subtract, None, "GA", "GS")
+        ts(GA, T.XH[:, 7::8], -163840.0, 5.0, A.mult, A.add, "XH", "GA")
+        op("V", lambda: v.reciprocal(GS, GA), "GA", "GS")
         lastw["gs0"] = lastw["gs1"] = lastw["GS"]
         for k in range(8):
             for s in range(2):
                 c = 8 * s + k
-                op("V", lambda: v.tensor_reduce(T.RP[:, c:c + 1], T.GS[:, 16 * s:16 * s + 16], X, A.max, negate=True), "gs%d" % s, "rp%d" % c)
+                op("V", lambda: v.tensor_reduce(T.RP[:, c:c + 1], T.GS[:, 16 * s:16 * s + 16], X, A.min, negate=True), "gs%d" % s, "rp%d" % c)
             if k == 7:
                 break
             for s in range(2):
                 c = 8 * s + k
-                ts(T.TM[:, 16 * s:16 * s + 16], T.E[:, 128 * s + k:128 * s + 128:8], T.RP[:, c:c + 1], 0.062 * 0.25 ** k - 1.0, A.max, A.add,
+                ts(T.TM[:, 16 * s:16 * s + 16], T.E[:, 128 * s + k:128 * s + 128:8], T.RP[:, c:c + 1], 0.062 * 0.25 ** k, A.min, A.subtract,
                    "E rp%d" % c, "tm%d" % s)
             for s in range(2):
                 a = T.GS[:, 16 * s:16 * s + 16]
-                tt(a, a, T.TM[:, 16 * s:16 * s + 16], A.min, "gs%d tm%d" % (s, s), "gs%d" % s)
+                tt(a, a, T.TM[:, 16 * s:16 * s + 16], A.max, "gs%d tm%d" % (s, s), "gs%d" % s)
         K = T.KK[:, 0:16]
-        tt(K, T.RP[:], T.TK[:], A.is_lt, "TK " + " ".join("rp%d" % c for c in range(16)), "K")
+        tt(K, T.RP[:], T.TK[:], A.is_gt, "TK " + " ".join("rp%d" % c for c in range(16)), "K")
         tt(T.KK[:, 16:32], K, T.SG[:, 0:16], A.mult, "K SG", "KA")
         tt(T.KK[:, 32:48], K, T.SG[:, 16:32], A.mult, "K SG", "KB")
         tt(T.KK[:, 48:64], K, T.SG[:, 32:48], A.mult, "K SG", "KC")
@@ -430,17 +453,16 @@ def rank_program(g, core, T, topo):
                 n, e, o = 256 >> k, 256 * (8 * s + k + 1), 774 * s + 256 + so[k]
                 scan(T.XO[:, e - n:e], T.RS[:, o:o + n], T.O[:, 256 * s + (1 << k) - 1:256 * s + 256:1 << k], -65536.0, A.add, A.max, "RS O%d" % s, "", "XO")
         K2 = T.KK[:, 64:80]
-        ts(K2, K, 256.0, None, A.mult, None, "K", "K2")
+        ts(K2, K, 16384.0, None, A.mult, None, "K", "K2")
         ts(T.YI[:, 0:16], T.XO[:, 255::256], -1.0, 4096.0, A.mult, A.add, "XO", "Y0")
         ts(T.YI[:, 16:32], T.YI[:, 0:16], 8191, None, A.bitwise_and, None, "Y0", "Y1")
         for s in range(2):
             ts(T.YI[:, 48 + 8 * s:56 + 8 * s], T.YI[:, 16 + 8 * s:24 + 8 * s], 4096.0, sc(7 + 8 * s), A.min, A.add, "Y1 s7 s15", "", "YJ")
-        ts(T.YI[:, 0:16], T.YI[:, 48:64], 255, None, A.bitwise_and, None, "YJ", "Y0")
         g0 = 3 * t % 8
         for s in range(2):
             for a, b, c in ((0, 8 - g0, g0), (8 - g0, 8, 0)):
                 if a < b:
-                    tt(T.YT[:, 16 * s + c:16 * s + c + b - a], T.YI[:, 8 * s + a:8 * s + b], T.KK[:, 64 + 8 * s + a:64 + 8 * s + b], A.add, "Y0 K2", "", "YT")
+                    tt(T.YT[:, 16 * s + c:16 * s + c + b - a], T.YI[:, 48 + 8 * s + a:48 + 8 * s + b], T.KK[:, 64 + 8 * s + a:64 + 8 * s + b], A.add, "YJ K2", "", "YT")
         op("V", lambda: v.transpose(T.YT[:, 32:64], T.YT[:, 0:32]), "YT", "TR")
         LB, lb = T["LB%d" % t], "LB%d" % t
         for q in range(8):
@@ -448,11 +470,10 @@ def rank_program(g, core, T, topo):
         if t == 0:
             setup_f()
         L = T.LF
-        ts(L[:, 0:16], LB[:], 256.0, 256.0, A.is_ge, A.mult, lb, "l0")
-        ts(T.DL[:, 0:16], LB[:], 256.0, None, A.is_lt, None, lb + " DL", "dl")
-        tt(T.AF[:, 0:16], LB[:], L[:, 0:16], A.subtract, lb + " l0 AF", "af")
+        ts(T.DL[:, 0:16], LB[:], 16384.0, None, A.is_lt, None, lb + " DL", "dl")
+        ts(T.AI[:], LB[:], 255, None, A.bitwise_and, None, lb, "ai")
         op("V", lambda: v.transpose(T.DL[:, 32:64], T.DL[:, 0:32]), "dl", "dt")
-        cp(T.AU[:], T.AF[:, 0:16], "af", "AU")
+        cp(T.AU[:], T.AI[:], "ai", "AU")
         scan(T.WC[:, 0:32], T.H10[:, 0:32], T.DL[:, 32:64], 0.0, A.mult, A.add, "H10 dt", "w0")
 
         def mean(b):
@@ -466,19 +487,18 @@ def rank_program(g, core, T, topo):
         tt(L[:, 32:48], L[:, 16:32], JL, A.add, "l1 JL", "l2")
         Wi, Cn, Bi = T.WC[:, 64:80], T.WC[:, 96:112], T.WC[:, 128:144]
         scan(Bi, T.NEG[:, 0:16], Cn, 0.0, A.max, A.add, "wt NEG", "bi")
+        tt(L[:, 48:64], Wi, Cn, A.subtract, "wt", "l3")
         mean(1)
-        tt(L[:, 48:64], Bi, Cn, A.subtract, "bi wt", "l3")
-        tt(L[:, 64:80], L[:, 48:64], Wi, A.add, "l3 wt", "l4")
-        ts(L[:, 80:96], L[:, 64:80], 1.0, None, A.subtract, None, "l4", "l5")
+        tt(L[:, 64:80], L[:, 48:64], Bi, A.add, "l3 bi", "l4")
+        ts(L[:, 80:96], L[:, 64:80], 1.0, T.WC[:, 143:144], A.subtract, A.subtract, "l4 bi", "l5")
         tt(L[:, 96:112], L[:, 32:48], L[:, 64:80], A.subtract, "l2 l4", "l6")
-        ts(L[:, 112:128], L[:, 96:112], T.WC[:, 143:144], None, A.add, None, "l6 bi", "l7")
-        tt(L[:, 128:144], L[:, 80:96], L[:, 112:128], A.max, "l5 l7", "pos")
-        cp(T.PU[:], L[:, 128:144], "pos", "PU")
+        tt(L[:, 112:128], L[:, 80:96], L[:, 96:112], A.max, "l5 l6", "l7")
+        ts(T.PU[:], L[:, 112:128], T.WC[:, 143:144], None, A.add, None, "l7 bi", "PU")
         mean(2)
         op("V", lambda: v.tensor_copy(T.LR[:].indirect(T.PU[:]), T.ICOL[:, 0:256]), "PU ICOL", "LR")
-        tt(T.LM[:, 0:96], T.LR[:, 0:96], T.MK[:], A.mult, "LR MK", "lm")
-        scan(T.LM[:, 96:192], T.H10[:], T.LM[:, 0:96], 0.0, A.mult, A.add, "H10 lm", "ln")
-        cp(T.LU[:, 0:6], T.LM[:, 111::16], "ln", "LU")
+        ts(L[:, 128:144], L[:, 112:128], T.WC[:, 143:144], None, A.add, None, "l7 bi", "pos")
+        scan(T.LM[:], T.MK[:, 0:96], T.LR[:, 0:96], 0.0, A.add, A.max, "MK LR", "ln")
+        ts(T.LU[:, 0:6], T.LM[:, 15::16], T.MK[:, 111:112], None, A.subtract, None, "ln MK", "LU")
         mean(3)
         for b in range(4):
             o, i = T.ET[:, b:384:4], T.XW[:, 352 * b:352 * b + 256].indirect(T.LU[:, 0:6])
@@ -496,6 +516,7 @@ def rank_program(g, core, T, topo):
         tt(L[:, 176:192], L[:, 160:176], JL, A.add, "m3 JL", "m2")
         cp(T.SU[:], L[:, 176:192], "m2", "SU")
         if last:
+            cp(T.AF[:, 0:16], T.AI[:], "ai AF", "af")
             op("V", lambda: v.transpose(T.AF[:, 32:64], T.AF[:, 0:32]), "af", "at")
             for q in range(8):
                 p = 32 * (q // 2)
@@ -512,18 +533,16 @@ def rank_program(g, core, T, topo):
                 act(o, i, kb, "XT%d" % b, scale=0.03125)
             else:
                 ts(o, i, 0.03125, None, A.mult, None, kb, "XT%d" % b)
-        for b in range(4):
             o, i = T.XT[:, b::4], T.XW[:, 352 * b:352 * b + 352].indirect(T.SU[:])
             if b % 2 == 0:
                 op("A", lambda: ac.activation(o, i, AF.Copy), "XZ%d XT%d SU" % (b, b), "", "XT")
             else:
                 op("V", lambda: v.tensor_copy(o, i), "XZ%d XT%d SU" % (b, b), "", "XT")
-    quant(T.XQ[:], T.XS[:], T.XT[:], "XT", "XQ XS")
-    quant(T.VQ[:], T.VS[:], T.VT[:], "VT", "VQ VS")
-    dma("Y", T.oc[:], T.XQ[:].bitcast(dt.uint8), "dout", "XQ")
+    quant(T.XQ[:], T.XS[:], T.XT[:], "XT", "XQ0 XQ1")
+    dma("Y", T.oc[:], T.XQ[:].bitcast(dt.uint8), "dout", "XQ0 XQ1")
     for k in range(4):
-        dma("A", T.osc[4 * k:4 * k + 4, :], T.XS[32 * k:32 * k + 4, :], "dout", "XS")
-    mm(B(3)[:, 0:256], T.VQ[:], T.VS[:], T.XQ[:], T.XS[:], True, True, "VQ VS XQ XS", "B3")
+        dma("A", T.osc[4 * k:4 * k + 4, :], T.XS[32 * k:32 * k + 4, :], "dout", "XQ0 XQ1")
+    mm(B(3)[:, 0:256], T.VQ[:], T.VS[:], T.XQ[:], T.XS[:], True, True, "VQ VS XQ0 XQ1", "B3")
     cp(T.YO[:], B(3)[:, 0:256], "B3", "YO")
     dma("Y", T.y[:], T.YO[:], "dout", "YO")
     for s in sorted(tot):

@@ -19,7 +19,7 @@ for _n, _w, _d in [
         ("OT", 1024, BF), ("OQ", 256, F8), ("OS", 256, U8), ("DS", 1024, F32), ("DT", 1024, BF), ("DQ", 256, F8), ("DP", 256, U8),
         ("HI", 192, BF), ("E", 256, BF), ("XH", 256, F32), ("GS", 64, F32), ("TM", 32, F32),
         ("RP", 16, F32), ("KK", 96, F32), ("AL", 24, F32), ("INC", 512, F32), ("O", 512, F32), ("XO", 4096, F32),
-        ("YI", 64, I32), ("YT", 64, I32), ("AI", 16, I32),
+        ("YI", 64, I32), ("YT", 64, I32), ("AI", 48, I32),
         ("LF", 192, F32), ("DL", 64, F32), ("AF", 64, F32), ("WC", 160, F32), ("AU", 16, U16), ("PU", 16, U16), ("LU", 8, U16), ("SU", 16, U16),
         ("LR", 256, F32), ("LM", 96, F32), ("HP", 2048, BF), ("XW", 1408, BF), ("ET", 512, BF), ("YO", 256, F32)]:
     SCRATCH[_n] = ("sbuf", [128, _w], _d)
@@ -174,13 +174,15 @@ def rank_program(g, core, T, topo):
     iota(T.IP[:, 0:1], [[0, 1]], 0, 1, "ip0", False)
     iota(T.UI[:], [[3, 3], [0, 8]], 0, 1, "UI", False)
     iota(T.ICOL[:], [[1, 512]], 0, 0, "ICOL")
+    iota(T.SC[:, 0:1], [[0, 1]], 0, 1, "s0")
+    iota(T.SC[:, 4:5], [[0, 1]], 128, 1, "s4")
+    iota(T.SC[:, 5:7], [[-128, 2]], 255, -1, "s5 s6")
     iota(T.I8[:], [[1, 16], [0, 8]], 0, 0, "I8")
     iota(T.I16[:], [[0, 8], [1, 16]], 0, 0, "I16")
     iota(T.JP[:, 0:128], [[4, 4], [1, 2], [16, 16]], 0, 0, "JP0")
     iota(T.JP[:, 128:256], [[4, 4], [1, 2], [16, 16]], 2, 0, "JP1")
     iota(T.VB[:], [[1, 256]], 0, 0, "VB")
     iota(T.PLF[:], [[-2, 2], [-4, 4], [-1, 2]], 255, 0, "PLF")
-    iota(T.IP[:, 8:10], [[128, 2]], 0, 1, "WI", False)
     iota(T.JL[:, 16:32], [[16, 16]], 0, 0, "JLF")
     iota(T.NEG[:], [[0, 256]], -1, 0, "NEG")
 
@@ -200,7 +202,6 @@ def rank_program(g, core, T, topo):
         fill(T.TK[:, k::8], 0.05 * 0.25 ** k, "", "TK")
     for nm, c, n in (("H50", 0.5, 8), ("H25", 0.25, 8), ("H8", 1.0, 8), ("H10", 1.0, 16)):
         fill(T[nm][:], c, nm)
-        fill(T[nm][:, 0::n], 0.0, nm)
     for st, n in ((1, 2), (2, 4), (4, 8), (8, 16)):
         fill(T.ILF[:, st:32:n], {1: 1.0, 2: 2.0, 4: 3.0, 8: 4.0}[st], "", "ILF")
     fill(T.ILF[:, 0:1], 13.0, "", "ILF")
@@ -209,18 +210,19 @@ def rank_program(g, core, T, topo):
     for nm in ("AL", "DL", "AF", "BT", "OT"):
         fill(T[nm][:], 0.0, nm)
     fill(T.ET[:, 384:512], 0.0, "ET4")
+    for nm, n in (("H50", 8), ("H25", 8), ("H8", 8), ("H10", 16)):
+        fill(T[nm][:, 0::n], 0.0, nm)
     flat("CMT", 1024, 0.0)
     flat("COT", 1024, 0.0)
     IP, SC = T.IP, T.SC
     for c, m in ((1, 15), (4, 1), (5, 3), (6, 7)):
         ts(IP[:, c:c + 1], IP[:, 0:1], m, None, A.bitwise_and, None, "ip0", "ip%d" % c)
-    for c, m in ((2, 4), (3, 5)):
+    for c, m in ((2, 4),):
         ts(IP[:, c:c + 1], IP[:, 0:1], m, None, A.arith_shift_right, None, "ip0", "ip%d" % c)
 
     def sc(c):
         return SC[:, c:c + 1]
-    for c, i, m, a in ((0, 0, 1.0, 0.0), (1, 1, 1.0, 0.0), (2, 2, 1.0, 0.0), (3, 2, 1.0, 8.0), (4, 0, 1.0, 128.0),
-                       (5, 0, -1.0, 255.0), (6, 0, -1.0, 127.0), (10, 1, 16.0, 0.0)):
+    for c, i, m, a in ((1, 1, 1.0, 0.0), (2, 2, 1.0, 0.0), (3, 2, 1.0, 8.0), (10, 1, 16.0, 0.0)):
         ts(sc(c), IP[:, i:i + 1], m, a, A.mult, A.add, "ip%d" % i, "s%d" % c)
     ts(T.UI[:], T.UI[:], 7, None, A.bitwise_and, None, "UI", "UI")
     ts(T.UL[:], T.UI[:], 16, None, A.mult, None, "UI", "UL")
@@ -238,12 +240,12 @@ def rank_program(g, core, T, topo):
         ones("EQT", so[k], 1, DEAD)
     ones("EQT", so[7] + 2, 1, DEAD)
     epoch["EQT"] = list(lastw["EQT"])
-    for o, n, c in ((129, 127, 0.0), (773, 1, 0.0), (775, 127, 0.0), (1030, 512, 0.0), (1542, 6, 0.0), (128, 1, -256.0), (774, 1, -256.0)):
+    for o, n, c in ((129, 127, 0.0), (256, 512, 0.0), (768, 6, 0.0), (775, 127, 0.0), (1030, 512, 0.0), (1542, 6, 0.0), (128, 1, -256.0), (774, 1, -256.0)):
         ones("TB", o, n, c)
     epoch["TB"] = list(lastw["TB"])
     for k in range(8):
         ones("TB", 1030 + so[k] + (1 if k == 7 else 0), 1, DEAD)
-    epoch["tb1"] = list(lastw["TB"])
+    epoch["tb1"] = epoch["tb0"] = list(lastw["TB"])
     flat("HMT", 1024, 0.0)
     ts(T.TH[:], T.I8[:], sc(1), 1e29, A.not_equal, A.mult, "I8 s1", "TH")
     for h in range(2):
@@ -258,28 +260,34 @@ def rank_program(g, core, T, topo):
     fill(T.H50[:], 0.5, "H50")
     fill(T.H50[:, 0::8], 0.0, "H50")
 
-    def setup_b():
-        for s in range(2):
-            if True:
-                ts(T.HMT[:, s::4], T.VB[:], sc(5 + s), 256.0, A.is_equal, A.mult, "VB s%d" % (5 + s), "", "HMT")
-        quant(T.HMQ[:], T.HMS[:], T.HMT[:], "HMT", "HMQ HMS")
-        ts(T.PL[:], T.PLF[:], sc(10), None, A.subtract, None, "PLF s10", "PL")
-        for b in range(4):
-            ts(T.MTT[:, b::4], T.VB[:], sc(0 if b < 2 else 4), None, A.is_equal, None, "VB s0 s4", "", "MTT")
-        quant(T.MTQ[:], T.MTS[:], T.MTT[:], "MTT", "MTQ MTS")
+    def setup_b(n):
+        if n < 2:
+            ts(T.HMT[:, n::4], T.VB[:], sc(5 + n), 256.0, A.is_equal, A.mult, "VB s%d" % (5 + n), "", "HMT")
+        elif n < 6:
+            ts(T.MTT[:, n - 2::4], T.VB[:], sc(0 if n < 4 else 4), None, A.is_equal, None, "VB s0 s4", "", "MTT")
+        elif n == 6:
+            ts(T.PL[:], T.PLF[:], sc(10), None, A.subtract, None, "PLF s10", "PL")
+        else:
+            quant(T.HMQ[:], T.HMS[:], T.HMT[:], "HMT", "HMQ HMS")
+            quant(T.MTQ[:], T.MTS[:], T.MTT[:], "MTT", "MTQ MTS")
 
     def setup_c():
-        for k in range(8):
-            ts(T.NI[:, k:16:8], T.IP[:, 8:10], k, None, A.arith_shift_right, None, "WI", "", "NI")
-        ts(T.NI[:, 16:32], T.NI[:, 0:16], 1, None, A.bitwise_and, None, "NI", "NB")
-        ts(T.NI[:, 32:48], T.NI[:, 16:32], -2, 1, A.mult, A.add, "NB", "NC")
-        tt(T.NS[:], T.NI[:, 0:16], T.NI[:, 32:48], A.add, "NI NC", "NS")
+        for k in range(7):
+            ts(T.NI[:, k:k + 1], IP[:, 0:1], k, None, A.arith_shift_right, None, "ip0", "", "NI")
         a = T.TB[:, 0:128]
         ts(a, T.VB[:, 0:128], sc(0), DEAD, A.is_equal, A.mult, "VB s0", "ta0")
+        ts(T.NI[:, 16:23], T.NI[:, 0:7], 1, None, A.bitwise_and, None, "NI", "NB")
+        setup_b(6)
+        ts(T.NI[:, 32:39], T.NI[:, 16:23], -2, 1, A.mult, A.add, "NB", "NC")
+        setup_b(5)
+        tt(T.NS[:, 0:7], T.NI[:, 0:7], T.NI[:, 32:39], A.add, "NI NC", "NS")
+        setup_b(2)
         for k in range(7):
             o, n = so[k] + 1, 128 >> k
             ts(T.EQT[:, o:o + n], T.VB[:, 0:n], T.NS[:, k:k + 1], DEAD, A.is_equal, A.mult, "VB NS", "", "EQT")
-        tt(T.TB[:, 256:773], T.EQT[:, 0:517], T.EQT[:, 1:518], A.subtract, "EQT", "tb0")
+        for k in range(8):
+            o, n = so[k], (128 >> k) + 1
+            tt(T.TB[:, 256 + o:256 + o + n], T.EQT[:, o:o + n], T.EQT[:, o + 1:o + n + 1], A.subtract, "EQT TB", "", "tb0")
         for k in range(7):
             o, n = 256 + so[k], 128 >> k
             i1, o1, i2, o2 = T.TB[:, o + 1:o + n], T.TB[:, 774 + o + n + 1:774 + o + 2 * n], T.TB[:, o:o + 1], T.TB[:, 774 + o + n:774 + o + n + 1]
@@ -290,6 +298,8 @@ def rank_program(g, core, T, topo):
             o, n = so[k] + 1, 128 >> k
             b = T.TB[:, 0:128:1 << k]
             tt(b, b, T.EQT[:, o:o + n], A.add, "EQT ta0", "ta0")
+            if k != 2 and k < 5:
+                setup_b(k)
         ts(a, a, -256.0 / DEAD, None, A.mult, None, "ta0", "ta0")
         act(T.TB[:, 902:1030], a, "ta0", "ta1")
         for h in range(2):
@@ -309,15 +319,11 @@ def rank_program(g, core, T, topo):
         quant(T.VQ[:], T.VS[:], T.VT[:], "VT", "VQ VS")
 
     def setup_d():
-        ts(sc(7), sc(10), sc(2), None, A.add, None, "s10 s2", "s7")
-        ts(sc(11), IP[:, 3:4], 2.0, None, A.mult, None, "ip3", "r0")
-        tt(sc(7), sc(7), sc(11), A.add, "s7 r0", "s7")
         for i in range(3):
             ts(sc(12 + i), IP[:, 4 + i:5 + i], 0.0, None, A.is_equal, None, "ip%d" % (4 + i), "r%d" % (1 + i))
         tt(sc(8), sc(12), sc(13), A.add, "r1 r2", "s8")
         tt(sc(8), sc(8), sc(14), A.add, "s8 r3", "s8")
         ts(sc(9), IP[:, 1:2], 0.0, None, A.is_equal, None, "ip1", "s9")
-        ts(sc(15), sc(7), 2.0, None, A.add, None, "s7", "s15")
         ts(T.ILF[:, 32:64], T.ILF[:, 0:32], sc(9), sc(8), A.mult, A.add, "ILF s9 s8", "ILG")
         cp(T.IL[:, 0:16], T.ILF[:, 32:48], "ILG", "IL0")
         ts(T.IL[:, 16:32], T.ILF[:, 48:64], 8.0, None, A.add, None, "ILG", "IL1")
@@ -355,25 +361,22 @@ def rank_program(g, core, T, topo):
             for s in range(2):
                 ts(T.PB[:, 8 * s:8 * s + 8], B(3 + s)[:, 0:8], 128.0, None, A.mult, None, "B%d" % (3 + s), "", "PB")
             scan(T.PB[:, 16:32], T.H50[:], T.PB[:, 0:16], 0.0, A.mult, A.add, "H50 PB", "PW")
-            ts(T.SG[:, 0:16], T.PB[:, 0:16], -128.0, 8192.0, A.mult, A.add, "PB", "", "SG")
             cp(T.IX[:], T.PB[:, 23::8], "PW", "IX")
-            ts(T.SG[:, 16:32], T.PB[:, 0:16], -256.0, 16384.0, A.mult, A.add, "PB", "", "SG")
-            ts(T.SG[:, 32:48], T.PB[:, 0:16], 64.0, None, A.mult, None, "PB", "", "SG")
+            for i, (a, b) in enumerate(((-128.0, 8192.0), (-256.0, 16384.0), (64.0, 0.0))):
+                op("A", lambda: ac.activation(T.SG[:, 16 * i:16 * i + 16], T.PB[:, 0:16], AF.Identity, bias=b, scale=a), "PB", "", "SG")
         if t == 0:
-            places()
             setup_c()
         scan(T.W8[:, 16:32], T.H50[:], T.W8[:, 0:16], 0.0, A.mult, A.add, "H50 W8", "WW")
         if t == 0:
-            setup_b()
+            setup_b(7)
         for s in range(2):
             ts(T.OT[:, s::4], T.VB[:], T.W8[:, 8 * s + 23:8 * s + 24], None, A.is_equal, None, "VB WW", "", "OT")
         quant(T.OQ[:], T.OS[:], T.OT[:], "OT", "OQ OS")
         for h in range(2):
             mm(B(5 + h)[:, 0:256], T.OQ[:, 128 * h:128 * h + 128], T.OS[:, 128 * h:128 * h + 128], T.HMQ[:], T.HMS[:], True, True, "OQ OS HMQ HMS", "B%d" % (5 + h))
+        places()
         if t == 0:
             setup_d()
-        else:
-            places()
         for h in range(2):
             scan(T.DS[:, 512 * h:512 * h + 256], T.NEG[:], B(5 + h)[:, 0:256], 0.0, A.add, A.max, "NEG B%d" % (5 + h), "DR%d" % h)
         for h in range(2):
@@ -383,8 +386,12 @@ def rank_program(g, core, T, topo):
         op("A", lambda: ac.activation(T.HT[:], D0, AF.Identity, bias=201326592.0), "DS0 PL", "HT")
         op("A", lambda: ac.activation(T.DT[:, 0::4], T.HT[:], AF.Identity, bias=-201326592.0), "HT", "dt0")
         ts(T.DT[:, 2::4], D1, 201326592.0, 201326592.0, A.add, A.subtract, "DS1 PL", "dt2")
-        tt(T.DT[:, 1::4], D0, T.DT[:, 0::4], A.subtract, "DS0 PL dt0", "dt1")
         tt(T.DT[:, 3::4], D1, T.DT[:, 2::4], A.subtract, "DS1 PL dt2", "dt3")
+        tt(T.DT[:, 1::4], D0, T.DT[:, 0::4], A.subtract, "DS0 PL dt0", "dt1")
+        WL = T["WL%d" % t]
+        HI, HI2, LO, GS = T.HI[:, 0:64], T.HI[:, 64:128], T.HI[:, 128:192], T.GS[:, 0:32]
+        ts(HI2, WL[:], 2.0, 2.0, A.is_ge, A.mult, "WL%d" % t, "HI2")
+        ts(HI, WL[:], 2.0, None, A.is_ge, None, "WL%d" % t, "HI")
         quant(T.DQ[:], T.DP[:], T.DT[:], "dt0 dt1 dt2 dt3", "DQ DP")
         for s in range(2):
             mm(B(s)[:, 0:256], T.DQ[:, 128 * s:128 * s + 128], T.DP[:, 128 * s:128 * s + 128], T.MTQ[:], T.MTS[:], True, True, "DQ DP MTQ MTS", "B%d" % s)
@@ -404,10 +411,6 @@ def rank_program(g, core, T, topo):
             flat("ELT", 2048, 0.0)
         else:
             halves()
-        WL = T["WL%d" % t]
-        HI, HI2, LO, GS = T.HI[:, 0:64], T.HI[:, 64:128], T.HI[:, 128:192], T.GS[:, 0:32]
-        ts(HI2, WL[:], 2.0, 2.0, A.is_ge, A.mult, "WL%d" % t, "HI2")
-        ts(HI, WL[:], 2.0, None, A.is_ge, None, "WL%d" % t, "HI")
         tt(LO, WL[:], HI2, A.subtract, "WL%d HI2" % t, "LO")
         for s in range(2):
             tt(T.E[:, 128 * s + 64:128 * s + 128], B(3 + s)[:, 64:128], HI, A.not_equal, "B%d HI" % (3 + s), "", "E")
@@ -452,17 +455,14 @@ def rank_program(g, core, T, topo):
             for k in range(8):
                 n, e, o = 256 >> k, 256 * (8 * s + k + 1), 774 * s + 256 + so[k]
                 scan(T.XO[:, e - n:e], T.RS[:, o:o + n], T.O[:, 256 * s + (1 << k) - 1:256 * s + 256:1 << k], -65536.0, A.add, A.max, "RS O%d" % s, "", "XO")
-        K2 = T.KK[:, 64:80]
-        ts(K2, K, 16384.0, None, A.mult, None, "K", "K2")
+        act(T.KK[:, 64:80], K, "K", "K2", scale=16384.0)
         ts(T.YI[:, 0:16], T.XO[:, 255::256], -1.0, 4096.0, A.mult, A.add, "XO", "Y0")
         ts(T.YI[:, 16:32], T.YI[:, 0:16], 8191, None, A.bitwise_and, None, "Y0", "Y1")
-        for s in range(2):
-            ts(T.YI[:, 48 + 8 * s:56 + 8 * s], T.YI[:, 16 + 8 * s:24 + 8 * s], 4096.0, sc(7 + 8 * s), A.min, A.add, "Y1 s7 s15", "", "YJ")
         g0 = 3 * t % 8
         for s in range(2):
             for a, b, c in ((0, 8 - g0, g0), (8 - g0, 8, 0)):
                 if a < b:
-                    tt(T.YT[:, 16 * s + c:16 * s + c + b - a], T.YI[:, 48 + 8 * s + a:48 + 8 * s + b], T.KK[:, 64 + 8 * s + a:64 + 8 * s + b], A.add, "YJ K2", "", "YT")
+                    tt(T.YT[:, 16 * s + c:16 * s + c + b - a], T.YI[:, 16 + 8 * s + a:16 + 8 * s + b], T.KK[:, 64 + 8 * s + a:64 + 8 * s + b], A.add, "Y1 K2", "", "YT")
         op("V", lambda: v.transpose(T.YT[:, 32:64], T.YT[:, 0:32]), "YT", "TR")
         LB, lb = T["LB%d" % t], "LB%d" % t
         for q in range(8):
@@ -471,35 +471,49 @@ def rank_program(g, core, T, topo):
             setup_f()
         L = T.LF
         ts(T.DL[:, 0:16], LB[:], 16384.0, None, A.is_lt, None, lb + " DL", "dl")
-        ts(T.AI[:], LB[:], 255, None, A.bitwise_and, None, lb, "ai")
+        ts(T.AI[:, 16:32], LB[:], 8191, None, A.bitwise_and, None, lb, "ai0")
         op("V", lambda: v.transpose(T.DL[:, 32:64], T.DL[:, 0:32]), "dl", "dt")
-        cp(T.AU[:], T.AI[:], "ai", "AU")
+        ts(T.AI[:, 32:48], T.AI[:, 16:32], 4096, None, A.min, None, "ai0", "ai1")
         scan(T.WC[:, 0:32], T.H10[:, 0:32], T.DL[:, 32:64], 0.0, A.mult, A.add, "H10 dt", "w0")
+        tt(T.AI[:, 16:32], T.AI[:, 32:48], T.JL[:, 0:16], A.add, "ai1 JL", "ai0")
 
         def mean(b):
-            tt(T.XW[:, 352 * b:352 * b + 256], T.HP[:, 256 * b:256 * b + 256].indirect(T.AU[:]), T.HP[:, 1024 + 256 * b:1280 + 256 * b], A.add, "HP AU", "XZ%d" % b)
-        mean(0)
+            b, h = divmod(b, 2)
+            o = 256 * b + 128 * h
+            tt(T.XW[:, o + 96 * b:o + 96 * b + 128], T.HP[:, 256 * b:256 * b + 256].indirect(T.AU[:, 8 * h:8 * h + 8]),
+               T.HP[:, 1024 + o:1152 + o], A.add, "HP AU", "", "XZ%d" % b)
         for i in range(2):
             ts(T.WC[:, 32 + 16 * i:48 + 16 * i], T.WC[:, 0:16], 0.0, T.WC[:, 16 * i + 15:16 * i + 16], A.mult, A.add, "w0", "w%d" % (1 + i))
+        ts(T.AI[:, 0:16], T.AI[:, 16:32], 255, None, A.bitwise_and, None, "ai0", "ai")
         op("V", lambda: v.transpose(T.WC[:, 64:128], T.WC[:, 0:64]), "w0 w1 w2", "wt")
-        ts(L[:, 16:32], T.DL[:, 0:16], -1024.0, None, A.mult, None, "dl", "l1")
+        cp(T.AU[:], T.AI[:, 0:16], "ai", "AU")
+        act(L[:, 16:32], T.DL[:, 0:16], "dl", "l1", scale=-1024.0)
         JL = T.JL[:, 0:16]
         tt(L[:, 32:48], L[:, 16:32], JL, A.add, "l1 JL", "l2")
         Wi, Cn, Bi = T.WC[:, 64:80], T.WC[:, 96:112], T.WC[:, 128:144]
         scan(Bi, T.NEG[:, 0:16], Cn, 0.0, A.max, A.add, "wt NEG", "bi")
         tt(L[:, 48:64], Wi, Cn, A.subtract, "wt", "l3")
-        mean(1)
+        mean(0)
         tt(L[:, 64:80], L[:, 48:64], Bi, A.add, "l3 bi", "l4")
+        mean(1)
         ts(L[:, 80:96], L[:, 64:80], 1.0, T.WC[:, 143:144], A.subtract, A.subtract, "l4 bi", "l5")
         tt(L[:, 96:112], L[:, 32:48], L[:, 64:80], A.subtract, "l2 l4", "l6")
-        tt(L[:, 112:128], L[:, 80:96], L[:, 96:112], A.max, "l5 l6", "l7")
-        ts(T.PU[:], L[:, 112:128], T.WC[:, 143:144], None, A.add, None, "l7 bi", "PU")
         mean(2)
+        tt(L[:, 112:128], L[:, 80:96], L[:, 96:112], A.max, "l5 l6", "l7")
+        mean(3)
+        ts(T.PU[:], L[:, 112:128], T.WC[:, 143:144], None, A.add, None, "l7 bi", "PU")
+        mean(4)
+        mean(5)
         op("V", lambda: v.tensor_copy(T.LR[:].indirect(T.PU[:]), T.ICOL[:, 0:256]), "PU ICOL", "LR")
         ts(L[:, 128:144], L[:, 112:128], T.WC[:, 143:144], None, A.add, None, "l7 bi", "pos")
+        ts(L[:, 144:160], L[:, 128:144], 96.0, None, A.is_lt, None, "pos", "m0")
+        tt(L[:, 160:176], L[:, 128:144], JL, A.subtract, "pos JL", "m1")
         scan(T.LM[:], T.MK[:, 0:96], T.LR[:, 0:96], 0.0, A.add, A.max, "MK LR", "ln")
+        ts(L[:, 176:192], L[:, 160:176], 256.0, None, A.add, None, "m1", "m2")
+        mean(6)
+        mean(7)
         ts(T.LU[:, 0:6], T.LM[:, 15::16], T.MK[:, 111:112], None, A.subtract, None, "ln MK", "LU")
-        mean(3)
+        tt(L[:, 160:176], L[:, 176:192], L[:, 144:160], A.mult, "m2 m0", "m3")
         for b in range(4):
             o, i = T.ET[:, b:384:4], T.XW[:, 352 * b:352 * b + 256].indirect(T.LU[:, 0:6])
             if b in (0, 2):
@@ -509,14 +523,10 @@ def rank_program(g, core, T, topo):
         quant(T.EQ[:], T.ES[:], T.ET[:], "ET ET4", "EQ ES")
         remote(T["AC%d" % t][:, 0:96].bitcast(dt.uint8), T.EQ[:, 0:96].bitcast(dt.uint8), "ca%d" % t, "lc%d" % t, "EQ", "AC%d" % t)
         remote(T["AS%d" % t][:, 0:96], T.ES[:, 0:96], "ca%d" % t, "lc%d" % t, "ES", "AS%d" % t)
-        ts(L[:, 144:160], L[:, 128:144], 96.0, None, A.is_lt, None, "pos", "m0")
-        tt(L[:, 160:176], L[:, 128:144], JL, A.subtract, "pos JL", "m1")
-        ts(L[:, 176:192], L[:, 160:176], 256.0, None, A.add, None, "m1", "m2")
-        tt(L[:, 160:176], L[:, 176:192], L[:, 144:160], A.mult, "m2 m0", "m3")
         tt(L[:, 176:192], L[:, 160:176], JL, A.add, "m3 JL", "m2")
         cp(T.SU[:], L[:, 176:192], "m2", "SU")
         if last:
-            cp(T.AF[:, 0:16], T.AI[:], "ai AF", "af")
+            cp(T.AF[:, 0:16], T.AI[:, 0:16], "ai AF", "af")
             op("V", lambda: v.transpose(T.AF[:, 32:64], T.AF[:, 0:32]), "af", "at")
             for q in range(8):
                 p = 32 * (q // 2)
@@ -529,13 +539,14 @@ def rank_program(g, core, T, topo):
             mm(B(DB[b])[:, 0:128], T.ELQ[:, 128 * b:128 * b + 128], T.ELS[:, 128 * b:128 * b + 128], AC[:], AS[:], False, True, "ELQ ELS AC%d AS%d" % (t, t), "", kb)
         for b in range(4):
             kb, o, i = "B%d" % DB[b], T.XW[:, 352 * b + 256:352 * b + 352], B(DB[b])[:, 0:96]
-            if b % 2 == 0:
-                act(o, i, kb, "XT%d" % b, scale=0.03125)
-            else:
-                ts(o, i, 0.03125, None, A.mult, None, kb, "XT%d" % b)
+            act(o, i, kb, "XT%d" % b, scale=0.03125)
+        for b in range(4):
             o, i = T.XT[:, b::4], T.XW[:, 352 * b:352 * b + 352].indirect(T.SU[:])
-            if b % 2 == 0:
-                op("A", lambda: ac.activation(o, i, AF.Copy), "XZ%d XT%d SU" % (b, b), "", "XT")
+            if b == 3:
+                o1, o2 = T.XT[:, 3:512:4], T.XT[:, 515::4]
+                i1, i2 = [T.XW[:, 1056:1408].indirect(T.SU[:, 8 * h:8 * h + 8]) for h in range(2)]
+                op("A", lambda: ac.activation(o1, i1, AF.Copy), "XZ3 XT3 SU", "", "XT")
+                op("V", lambda: v.tensor_copy(o2, i2), "XZ3 XT3 SU", "", "XT")
             else:
                 op("V", lambda: v.tensor_copy(o, i), "XZ%d XT%d SU" % (b, b), "", "XT")
     quant(T.XQ[:], T.XS[:], T.XT[:], "XT", "XQ0 XQ1")

from concourse.bass import IndirectOffsetOnAxis
from concourse.mybir import dt, AluOpType, AxisListType, ActivationFunctionType

F32, BF, I32, U16, F8, U8 = "float32", "bfloat16", "int32", "uint16", "float8_e4m3fn_x4", "uint8"
SCRATCH = {}
for _n, _w, _d in [
        ("X0", 1024, BF), ("UT", 512, BF), ("VT", 512, BF), ("WQ", 512, F8), ("WS", 512, U8),
        ("UQ", 128, F8), ("US", 128, U8), ("VQ", 128, F8), ("VS", 128, U8), ("URQ", 384, F8), ("URS", 384, U8),
        ("HT", 256, F32), ("ELT", 2048, BF), ("ELQ", 512, F8), ("ELS", 512, U8),
        ("CMT", 1024, BF), ("CMQ", 256, F8), ("CMS", 256, U8), ("COT", 1024, BF), ("COQ", 256, F8), ("COS", 256, U8),
        ("HMT", 1024, BF), ("HMQ", 256, F8), ("HMS", 256, U8), ("MTT", 1024, BF), ("MTQ", 256, F8), ("MTS", 256, U8),
        ("ICOL", 512, F32), ("VB", 256, BF), ("I8", 128, BF), ("I16", 128, BF), ("JP", 256, BF), ("TH", 128, F32),
        ("IP", 10, I32), ("SC", 16, F32), ("UI", 24, I32), ("UL", 24, U16), ("PLF", 16, F32), ("PL", 16, U16),
        ("ILF", 64, F32), ("IL", 32, U16), ("NI", 48, I32), ("NS", 16, F32),
        ("EQT", 518, BF), ("TB", 1548, BF), ("TK", 16, F32), ("H25", 256, BF), ("H50", 16, F32), ("H10", 96, F32),
        ("H8", 16, F32), ("NEG", 256, F32), ("JL", 32, F32), ("MK", 192, F32),
        ("XQ", 256, F8), ("XS", 256, U8), ("XT", 1024, BF), ("BT", 768, BF), ("BQ", 192, F8), ("BS", 192, U8),
        ("W8", 32, F32), ("PB", 32, F32), ("IX", 2, I32), ("SG", 48, F32), ("RS", 1548, BF),
        ("OT", 1024, BF), ("OQ", 256, F8), ("OS", 256, U8), ("DS", 1024, F32), ("DT", 1024, BF), ("DQ", 256, F8), ("DP", 256, U8),
        ("HI", 192, BF), ("E", 256, BF), ("XH", 256, F32), ("GS", 64, F32), ("TM", 32, F32),
        ("RP", 16, F32), ("KK", 96, F32), ("AL", 24, F32), ("INC", 512, F32), ("O", 512, F32), ("XO", 4096, F32),
        ("YI", 64, I32), ("YT", 64, I32), ("AI", 48, I32),
        ("LF", 192, F32), ("DL", 64, F32), ("AF", 64, F32), ("WC", 160, F32), ("AU", 16, U16), ("PU", 16, U16), ("LU", 8, U16), ("SU", 16, U16),
        ("LR", 256, F32), ("LM", 96, F32), ("HP", 2048, BF), ("XW", 1408, BF), ("ET", 512, BF), ("YO", 256, F32)]:
    SCRATCH[_n] = ("sbuf", [128, _w], _d)
for _t in range(3):
    SCRATCH["MS%d" % _t] = ("sbuf", [128, 64], BF)
    SCRATCH["WL%d" % _t] = ("sbuf", [128, 64], BF)
    SCRATCH["LB%d" % _t] = ("sbuf", [128, 16], I32)
    SCRATCH["AC%d" % _t] = ("sbuf", [128, 128], F8)
    SCRATCH["AS%d" % _t] = ("sbuf", [128, 128], U8)
    if _t == 0:
        SCRATCH["EQ"] = ("sbuf", [128, 128], F8)
        SCRATCH["ES"] = ("sbuf", [128, 128], U8)
for _b in range(8):
    SCRATCH["B%d" % _b] = ("psum", [128, 512], F32)
SCRATCH["tab"] = ("dram", [256, 774], BF)
SEMAPHORES = ["cV", "cA", "cP", "cG", "dx", "du", "dv", "dw", "dtab", "dfill", "dout"]
for _t in range(3):
    SEMAPHORES += ["wa%d" % _t, "ca%d" % _t, "lw%d" % _t, "lc%d" % _t, "dl%d" % _t, "di%d" % _t]


def rank_program(g, core, T, topo):
    rank = T.rank_of(core)
    if rank is None:
        return
    mate = T.cores[rank + 1 if rank % 2 == 0 else rank - 1]
    A, AF = AluOpType, ActivationFunctionType
    X = AxisListType.X
    Q = {"V": g.vector, "A": g.scalar, "P": g.tensor, "G": g, "Y": g.sync}
    own = {"V": "cV", "A": "cA", "P": "cP", "G": "cG", "Y": None}
    tot, lastw, readers, epoch, known = {}, {}, {}, {}, {e: {} for e in Q}

    def need(e, toks):
        for s, v in sorted(toks):
            n = tot[s] if v is None else v
            if known[e].get(s, 0) < n:
                Q[e].wait_ge(T.sem[s], n)
                known[e][s] = n

    def deps(e, r, w, add, compute):
        toks = {}

        def put(tk, war=False):
            s, v = tk
            if war and compute and s == own[e]:
                return
            n = tot[s] if v is None else v
            toks[s] = max(toks.get(s, 0), n)
        for k in r:
            for tk in lastw.get(k, []):
                put(tk)
            if k[0] == "B" and k[1:].isdigit():
                for tk in readers.get(k, []):
                    put(tk, True)
        for k in w:
            for tk in lastw.get(k, []):
                put(tk)
            for tk in readers.get(k, []):
                put(tk, True)
        for k in add:
            if readers.get(k):
                epoch[k] = lastw.get(k, []) + readers[k]
                lastw[k], readers[k] = [], []
            for tk in epoch.get(k, []):
                put(tk)
        need(e, list(toks.items()))

    def note(tk, r, w, add):
        for k in r:
            readers.setdefault(k, []).append(tk)
        for k in w:
            lastw[k], readers[k], epoch[k] = [tk], [], [tk]
        for k in add:
            lastw.setdefault(k, []).append(tk)

    def op(e, f, r, w=(), add=()):
        r, w, add = r.split(), (w.split() if w else []), (add.split() if add else [])
        deps(e, r, w, add, True)
        s = own[e]
        f().then_inc(T.sem[s], 1)
        tot[s] = tot.get(s, 0) + 1
        note((s, tot[s]), r, w, add)

    def dma(e, out, in_, s, r, w="", add=""):
        r, w, add = r.split(), w.split(), add.split()
        deps(e, r, w, add, False)
        Q[e].dma_start(out, in_).then_inc(T.sem[s], 16)
        tot[s] = tot.get(s, 0) + 16
        note((s, None), r, w, add)

    eng = topo.engines(core, mate)
    ne = 1
    while ne * 2 <= len(eng):
        ne *= 2
    msk = 0
    for _e in eng[:ne]:
        msk |= 1 << _e
    rid, pid = topo.addr(mate)[:2]

    def remote(out, in_, rs, ls, r, w):
        deps("G", r.split(), [], [], False)
        g.remote_dma(out_ap=out, in_ap=in_, remote_sem=T.sem[rs], local_sem=T.sem[ls], pid=pid, routing_id=rid, dma_engine_mask=msk)
        tot[ls] = tot.get(ls, 0) + ne
        tot[rs] = tot.get(rs, 0) + ne
        note((ls, None), r.split(), [], [])
        for k in w.split():
            lastw.setdefault(k, []).append((rs, None))

    v, ac, pe = g.vector, g.scalar, g.tensor

    def ts(out, in0, s1, s2, o0, o1, r, w="", add=""):
        if o1 is None:
            op("V", lambda: v.tensor_scalar(out, in0, s1, None, o0), r, w, add)
        else:
            op("V", lambda: v.tensor_scalar(out, in0, s1, s2, o0, o1), r, w, add)

    def tt(out, a, b, o, r, w="", add=""):
        op("V", lambda: v.tensor_tensor(out, a, b, o), r, w, add)

    def cp(out, a, r, w="", add=""):
        op("V", lambda: v.tensor_copy(out, a), r, w, add)

    def scan(out, d0, d1, ini, o0, o1, r, w="", add=""):
        op("V", lambda: v.tensor_tensor_scan(out, d0, d1, ini, o0, o1), r, w, add)

    def fill(ap, c, w="", add=""):
        op("V", lambda: v.memset(ap, c), "", w, add)

    def quant(c, s, t, r, w):
        op("V", lambda: v.quantize_mx(c, s, t), r, w)

    def act(out, in_, r, w="", add="", scale=1.0):
        if scale == 1.0:
            op("A", lambda: ac.activation(out, in_, AF.Copy), r, w, add)
        else:
            op("A", lambda: ac.activation(out, in_, AF.Copy, scale=scale), r, w, add)

    def mm(out, l, ls, rr, rs, a, z, r, w="", add=""):
        op("P", lambda: pe.matmul_mx(out, l, ls, rr, rs, a, z), r, w, add)

    def iota(out, pat, base, ch, w, flag=True):
        if flag:
            op("G", lambda: g.iota(out, pat, base, ch, allow_small_or_imprecise_dtypes=True), "", w)
        else:
            op("G", lambda: g.iota(out, pat, base, ch), "", w)

    dma("Y", T.X0[:], T.x[:], "dx", "", "X0")
    dma("A", T.UT[:], T.u[:], "du", "", "UT")
    dma("Y", T.WQ[:].bitcast(dt.uint8), T.wc[:], "dw", "", "WQ")
    dma("Y", T.WS[:], T.ws[:], "dw", "", "WS")
    dma("A", T.VT[:], T.v[:], "dv", "", "VT")

    iota(T.IP[:, 0:1], [[0, 1]], 0, 1, "ip0", False)
    iota(T.UI[:], [[3, 3], [0, 8]], 0, 1, "UI", False)
    iota(T.ICOL[:], [[1, 512]], 0, 0, "ICOL")
    iota(T.SC[:, 0:1], [[0, 1]], 0, 1, "s0")
    iota(T.SC[:, 4:5], [[0, 1]], 128, 1, "s4")
    iota(T.SC[:, 5:7], [[-128, 2]], 255, -1, "s5 s6")
    iota(T.I8[:], [[1, 16], [0, 8]], 0, 0, "I8")
    iota(T.I16[:], [[0, 8], [1, 16]], 0, 0, "I16")
    iota(T.JP[:, 0:128], [[4, 4], [1, 2], [16, 16]], 0, 0, "JP0")
    iota(T.JP[:, 128:256], [[4, 4], [1, 2], [16, 16]], 2, 0, "JP1")
    iota(T.VB[:], [[1, 256]], 0, 0, "VB")
    iota(T.PLF[:], [[-2, 2], [-4, 4], [-1, 2]], 255, 0, "PLF")
    iota(T.JL[:, 16:32], [[16, 16]], 0, 0, "JLF")
    iota(T.NEG[:], [[0, 256]], -1, 0, "NEG")

    DEAD = 262144.0

    def flat(nm, width, c):
        for a in range(0, width, 512):
            b = min(width, a + 512)
            o, i = T[nm][:, a:b], T.ICOL[:, 0:b - a]
            if c == 0.0:
                op("A", lambda: ac.activation(o, i, AF.Copy, scale=0.0), "ICOL", "", nm)
            else:
                op("A", lambda: ac.activation(o, i, AF.Identity, bias=c, scale=0.0), "ICOL", "", nm)
        epoch[nm] = list(lastw[nm])

    for k in range(8):
        fill(T.TK[:, k::8], 0.05 * 0.25 ** k, "", "TK")
    for nm, c, n in (("H50", 0.5, 8), ("H25", 0.25, 8), ("H8", 1.0, 8), ("H10", 1.0, 16)):
        fill(T[nm][:], c, nm)
    for st, n in ((1, 2), (2, 4), (4, 8), (8, 16)):
        fill(T.ILF[:, st:32:n], {1: 1.0, 2: 2.0, 4: 3.0, 8: 4.0}[st], "", "ILF")
    fill(T.ILF[:, 0:1], 13.0, "", "ILF")
    fill(T.ILF[:, 16:17], 6.0, "", "ILF")
    fill(T.YT[:], 0, "YT")
    for nm in ("AL", "DL", "AF", "BT", "OT"):
        fill(T[nm][:], 0.0, nm)
    fill(T.ET[:, 384:512], 0.0, "ET4")
    for nm, n in (("H50", 8), ("H25", 8), ("H8", 8), ("H10", 16)):
        fill(T[nm][:, 0::n], 0.0, nm)
    flat("CMT", 1024, 0.0)
    flat("COT", 1024, 0.0)
    IP, SC = T.IP, T.SC
    for c, m in ((1, 15), (4, 1), (5, 3), (6, 7)):
        ts(IP[:, c:c + 1], IP[:, 0:1], m, None, A.bitwise_and, None, "ip0", "ip%d" % c)
    for c, m in ((2, 4),):
        ts(IP[:, c:c + 1], IP[:, 0:1], m, None, A.arith_shift_right, None, "ip0", "ip%d" % c)

    def sc(c):
        return SC[:, c:c + 1]
    for c, i, m, a in ((1, 1, 1.0, 0.0), (2, 2, 1.0, 0.0), (3, 2, 1.0, 8.0), (10, 1, 16.0, 0.0)):
        ts(sc(c), IP[:, i:i + 1], m, a, A.mult, A.add, "ip%d" % i, "s%d" % c)
    ts(T.UI[:], T.UI[:], 7, None, A.bitwise_and, None, "UI", "UI")
    ts(T.UL[:], T.UI[:], 16, None, A.mult, None, "UI", "UL")
    quant(T.UQ[:], T.US[:], T.UT[:], "UT", "UQ US")
    cp(T.URQ[:].bitcast(dt.uint32), T.UQ[:].bitcast(dt.uint32).indirect(T.UL[:]), "UQ UL", "URQ")
    op("A", lambda: ac.activation(T.URS[:], T.US[:].indirect(T.UL[:]), AF.Copy), "US UL", "URS")
    so = [0]
    for k in range(8):
        so.append(so[-1] + 1 + (256 >> k))

    def ones(nm, o, n, c):
        op("A", lambda: ac.activation(T[nm][:, o:o + n], T.ICOL[:, 0:n], AF.Identity, bias=c, scale=0.0), "ICOL", "", nm)
    flat("EQT", 518, 0.0)
    for k in range(8):
        ones("EQT", so[k], 1, DEAD)
    ones("EQT", so[7] + 2, 1, DEAD)
    epoch["EQT"] = list(lastw["EQT"])
    for o, n, c in ((129, 127, 0.0), (256, 512, 0.0), (768, 6, 0.0), (775, 127, 0.0), (1030, 512, 0.0), (1542, 6, 0.0), (128, 1, -256.0), (774, 1, -256.0)):
        ones("TB", o, n, c)
    epoch["TB"] = list(lastw["TB"])
    for k in range(8):
        ones("TB", 1030 + so[k] + (1 if k == 7 else 0), 1, DEAD)
    epoch["tb1"] = epoch["tb0"] = list(lastw["TB"])
    flat("HMT", 1024, 0.0)
    ts(T.TH[:], T.I8[:], sc(1), 1e29, A.not_equal, A.mult, "I8 s1", "TH")
    for h in range(2):
        for b in range(2):
            ts(T.CMT[:, 512 * h + b:512 * h + 512:4], T.I16[:], sc(2 + b), float(1 + h), A.is_equal, A.mult, "I16 s%d" % (2 + b), "", "CMT")
    for s in range(2):
        for b in range(2):
            ts(T.COT[:, 512 * s + 2 + b:512 * s + 512:4], T.JP[:, 128 * s:128 * s + 128], sc(0 if b == 0 else 4), None, A.is_equal, None,
               "JP%d s0 s4" % s, "", "COT")
    quant(T.CMQ[:], T.CMS[:], T.CMT[:], "CMT", "CMQ CMS")
    quant(T.COQ[:], T.COS[:], T.COT[:], "COT", "COQ COS")
    fill(T.H50[:], 0.5, "H50")
    fill(T.H50[:, 0::8], 0.0, "H50")

    def setup_b(n):
        if n < 2:
            ts(T.HMT[:, n::4], T.VB[:], sc(5 + n), 256.0, A.is_equal, A.mult, "VB s%d" % (5 + n), "", "HMT")
        elif n < 6:
            ts(T.MTT[:, n - 2::4], T.VB[:], sc(0 if n < 4 else 4), None, A.is_equal, None, "VB s0 s4", "", "MTT")
        elif n == 6:
            ts(T.PL[:], T.PLF[:], sc(10), None, A.subtract, None, "PLF s10", "PL")
        else:
            quant(T.HMQ[:], T.HMS[:], T.HMT[:], "HMT", "HMQ HMS")
            quant(T.MTQ[:], T.MTS[:], T.MTT[:], "MTT", "MTQ MTS")

    def setup_c():
        for k in range(7):
            ts(T.NI[:, k:k + 1], IP[:, 0:1], k, None, A.arith_shift_right, None, "ip0", "", "NI")
        a = T.TB[:, 0:128]
        ts(a, T.VB[:, 0:128], sc(0), DEAD, A.is_equal, A.mult, "VB s0", "ta0")
        ts(T.NI[:, 16:23], T.NI[:, 0:7], 1, None, A.bitwise_and, None, "NI", "NB")
        setup_b(6)
        ts(T.NI[:, 32:39], T.NI[:, 16:23], -2, 1, A.mult, A.add, "NB", "NC")
        setup_b(5)
        tt(T.NS[:, 0:7], T.NI[:, 0:7], T.NI[:, 32:39], A.add, "NI NC", "NS")
        setup_b(2)
        for k in range(7):
            o, n = so[k] + 1, 128 >> k
            ts(T.EQT[:, o:o + n], T.VB[:, 0:n], T.NS[:, k:k + 1], DEAD, A.is_equal, A.mult, "VB NS", "", "EQT")
        for k in range(8):
            o, n = so[k], (128 >> k) + 1
            tt(T.TB[:, 256 + o:256 + o + n], T.EQT[:, o:o + n], T.EQT[:, o + 1:o + n + 1], A.subtract, "EQT TB", "", "tb0")
        for k in range(7):
            o, n = 256 + so[k], 128 >> k
            i1, o1, i2, o2 = T.TB[:, o + 1:o + n], T.TB[:, 774 + o + n + 1:774 + o + 2 * n], T.TB[:, o:o + 1], T.TB[:, 774 + o + n:774 + o + n + 1]
            if n > 1:
                act(o1, i1, "tb0 TB", "", "tb1")
            op("A", lambda: ac.activation(o2, i2, AF.Identity, bias=-DEAD, scale=1.0), "tb0 TB", "", "tb1")
        for k in range(7):
            o, n = so[k] + 1, 128 >> k
            b = T.TB[:, 0:128:1 << k]
            tt(b, b, T.EQT[:, o:o + n], A.add, "EQT ta0", "ta0")
            if k != 2 and k < 5:
                setup_b(k)
        ts(a, a, -256.0 / DEAD, None, A.mult, None, "ta0", "ta0")
        act(T.TB[:, 902:1030], a, "ta0", "ta1")
        for h in range(2):
            dma("Y", T.tab[128 * h:128 * h + 128, :], T.TB[:, 774 * h:774 * h + 774], "dtab", "ta%d tb%d TB" % (h, h), "", "tab")

    def setup_e():
        for b in range(4):
            ts(T.ELT[:, 512 * b + b:512 * b + 512:4], T.VB[:, 0:128], sc(0), 32.0, A.is_equal, A.mult, "VB s0", "", "ELT")
        quant(T.ELQ[:], T.ELS[:], T.ELT[:], "ELT", "ELQ ELS")

    def setup_f():
        ts(T.JL[:, 0:16], T.JL[:, 16:32], sc(1), None, A.add, None, "JLF s1", "JL")
        ts(T.MK[:, 96:192], T.I16[:, 0:96], sc(1), 8000.0, A.not_equal, A.mult, "I16 s1", "mk0")
        tt(T.MK[:, 1:96], T.MK[:, 97:192], T.MK[:, 96:191], A.subtract, "mk0", "MK")
        ts(T.MK[:, 16:96:16], T.MK[:, 16:96:16], 3000.0, None, A.subtract, None, "MK", "MK")
        cp(T.MK[:, 0:1], T.MK[:, 96:97], "mk0 MK", "MK")
        quant(T.VQ[:], T.VS[:], T.VT[:], "VT", "VQ VS")

    def setup_d():
        for i in range(3):
            ts(sc(12 + i), IP[:, 4 + i:5 + i], 0.0, None, A.is_equal, None, "ip%d" % (4 + i), "r%d" % (1 + i))
        tt(sc(8), sc(12), sc(13), A.add, "r1 r2", "s8")
        tt(sc(8), sc(8), sc(14), A.add, "s8 r3", "s8")
        ts(sc(9), IP[:, 1:2], 0.0, None, A.is_equal, None, "ip1", "s9")
        ts(T.ILF[:, 32:64], T.ILF[:, 0:32], sc(9), sc(8), A.mult, A.add, "ILF s9 s8", "ILG")
        cp(T.IL[:, 0:16], T.ILF[:, 32:48], "ILG", "IL0")
        ts(T.IL[:, 16:32], T.ILF[:, 48:64], 8.0, None, A.add, None, "ILG", "IL1")

    def B(b):
        return T["B%d" % b]

    DB = (2, 5, 6, 7)
    for t in range(3):
        last = t == 2
        src, key = (T.X0, "X0") if t == 0 else (T.XT, "XT")
        for h in range(2):
            quant(T.XQ[:, 128 * h:128 * h + 128], T.XS[:, 128 * h:128 * h + 128], src[:, 512 * h:512 * h + 512], key, "XQ%d" % h)
        if t == 0:
            for i in range(3):
                dma("Y", T["AC%d" % i][:, 96:128].bitcast(dt.uint8), T.XQ[:, 0:32].bitcast(dt.uint8), "dfill", "XQ0", "", "AC%d" % i)
                dma("Y", T["AS%d" % i][:, 96:128], T.XS[:, 0:32], "dfill", "XQ0", "", "AS%d" % i)
        for s in range(2):
            mm(B(s)[:, 0:128], T.XQ[:, 128 * s:128 * s + 128], T.XS[:, 128 * s:128 * s + 128], T.URQ[:, 128 * t:128 * t + 128], T.URS[:, 128 * t:128 * t + 128],
               True, True, "XQ%d URQ URS" % s, "B%d" % s)
        for s in range(2):
            tt(T.BT[:, s:512:4], B(s)[:, 0:128], T.TH[:], A.is_gt, "B%d TH" % s, "", "BT")
            ts(T.BT[:, 2 + s:512:4], B(s)[:, 0:128], 0.0, None, A.is_gt, None, "B%d" % s, "", "BT")
        for s in range(2):
            ts(T.W8[:, 8 * s:8 * s + 8], B(s)[:, 0:8], 0.0, 128.0, A.is_gt, A.mult, "B%d" % s, "", "W8")
        quant(T.BQ[:], T.BS[:], T.BT[:], "BT", "BQ BS")
        mm(B(2)[:, 0:128], T.CMQ[:, 0:128], T.CMS[:, 0:128], T.BQ[:, 0:128], T.BS[:, 0:128], True, False, "CMQ CMS BQ BS", "B2")
        mm(B(2)[:, 0:128], T.CMQ[:, 128:256], T.CMS[:, 128:256], T.BQ[:, 64:192], T.BS[:, 64:192], False, True, "CMQ CMS BQ BS", "", "B2")
        for s in range(2):
            mm(B(3 + s)[:, 0:128], T.COQ[:, 128 * s:128 * s + 128], T.COS[:, 128 * s:128 * s + 128], T.BQ[:, 0:128], T.BS[:, 0:128], True, True,
               "COQ COS BQ BS", "B%d" % (3 + s))
        act(T["MS%d" % t][:], B(2)[:, 0:64], "B2", "MS%d" % t)
        remote(T["WL%d" % t][:], T["MS%d" % t][:], "wa%d" % t, "lw%d" % t, "MS%d" % t, "WL%d" % t)
        def places():
            for s in range(2):
                ts(T.PB[:, 8 * s:8 * s + 8], B(3 + s)[:, 0:8], 128.0, None, A.mult, None, "B%d" % (3 + s), "", "PB")
            scan(T.PB[:, 16:32], T.H50[:], T.PB[:, 0:16], 0.0, A.mult, A.add, "H50 PB", "PW")
            cp(T.IX[:], T.PB[:, 23::8], "PW", "IX")
            for i, (a, b) in enumerate(((-128.0, 8192.0), (-256.0, 16384.0), (64.0, 0.0))):
                op("A", lambda: ac.activation(T.SG[:, 16 * i:16 * i + 16], T.PB[:, 0:16], AF.Identity, bias=b, scale=a), "PB", "", "SG")
        if t == 0:
            setup_c()
        scan(T.W8[:, 16:32], T.H50[:], T.W8[:, 0:16], 0.0, A.mult, A.add, "H50 W8", "WW")
        if t == 0:
            setup_b(7)
        for s in range(2):
            ts(T.OT[:, s::4], T.VB[:], T.W8[:, 8 * s + 23:8 * s + 24], None, A.is_equal, None, "VB WW", "", "OT")
        quant(T.OQ[:], T.OS[:], T.OT[:], "OT", "OQ OS")
        for h in range(2):
            mm(B(5 + h)[:, 0:256], T.OQ[:, 128 * h:128 * h + 128], T.OS[:, 128 * h:128 * h + 128], T.HMQ[:], T.HMS[:], True, True, "OQ OS HMQ HMS", "B%d" % (5 + h))
        places()
        if t == 0:
            setup_d()
        for h in range(2):
            scan(T.DS[:, 512 * h:512 * h + 256], T.NEG[:], B(5 + h)[:, 0:256], 0.0, A.add, A.max, "NEG B%d" % (5 + h), "DR%d" % h)
        for h in range(2):
            scan(T.DS[:, 512 * h + 256:512 * h + 512], T.NEG[:], B(5 + h)[:, 0:256], T.DS[:, 512 * h + 255:512 * h + 256], A.add, A.max,
                 "NEG DR%d B%d" % (h, 5 + h), "DS%d" % h)
        D0, D1 = [T.DS[:, 512 * h + 256:512 * h + 512].indirect(T.PL[:]) for h in range(2)]
        op("A", lambda: ac.activation(T.HT[:], D0, AF.Identity, bias=201326592.0), "DS0 PL", "HT")
        op("A", lambda: ac.activation(T.DT[:, 0::4], T.HT[:], AF.Identity, bias=-201326592.0), "HT", "dt0")
        ts(T.DT[:, 2::4], D1, 201326592.0, 201326592.0, A.add, A.subtract, "DS1 PL", "dt2")
        tt(T.DT[:, 3::4], D1, T.DT[:, 2::4], A.subtract, "DS1 PL dt2", "dt3")
        tt(T.DT[:, 1::4], D0, T.DT[:, 0::4], A.subtract, "DS0 PL dt0", "dt1")
        WL = T["WL%d" % t]
        HI, HI2, LO, GS = T.HI[:, 0:64], T.HI[:, 64:128], T.HI[:, 128:192], T.GS[:, 0:32]
        ts(HI2, WL[:], 2.0, 2.0, A.is_ge, A.mult, "WL%d" % t, "HI2")
        ts(HI, WL[:], 2.0, None, A.is_ge, None, "WL%d" % t, "HI")
        quant(T.DQ[:], T.DP[:], T.DT[:], "dt0 dt1 dt2 dt3", "DQ DP")
        for s in range(2):
            mm(B(s)[:, 0:256], T.DQ[:, 128 * s:128 * s + 128], T.DP[:, 128 * s:128 * s + 128], T.MTQ[:], T.MTS[:], True, True, "DQ DP MTQ MTS", "B%d" % s)
        deps("G", ["IX", "tab"], ["RS"], [], False)
        for s in range(2):
            g.indirect_dma_start(T.RS[:, 774 * s:774 * s + 774], None, T.tab[:], IndirectOffsetOnAxis(ap=T.IX[:, s:s + 1], axis=0),
                                 bounds_check=255).then_inc(T.sem["di%d" % t], 16)
        tot["di%d" % t] = 32
        note(("di%d" % t, None), ["IX", "tab"], ["RS"], [])
        def halves():
            for b in range(4):
                kb = "B%d" % DB[b]
                mm(B(DB[b])[:, 0:256], T.ELQ[:, 128 * b:128 * b + 128], T.ELS[:, 128 * b:128 * b + 128], T.XQ[:], T.XS[:], True, True, "ELQ ELS XQ0 XQ1", kb)
                for a in range(2):
                    act(T.HP[:, 1024 * a + 256 * b:1024 * a + 256 * b + 256], B(DB[b])[:, 0:256], kb, "", "HP", scale=0.015625)
        if t == 0:
            flat("ELT", 2048, 0.0)
        else:
            halves()
        tt(LO, WL[:], HI2, A.subtract, "WL%d HI2" % t, "LO")
        for s in range(2):
            tt(T.E[:, 128 * s + 64:128 * s + 128], B(3 + s)[:, 64:128], HI, A.not_equal, "B%d HI" % (3 + s), "", "E")
        for s in range(2):
            tt(T.E[:, 128 * s:128 * s + 64], B(3 + s)[:, 0:64], LO, A.not_equal, "B%d LO" % (3 + s), "", "E")
        scan(T.XH[:], T.H25[:], T.E[:], 0.0, A.mult, A.add, "H25 E", "XH")
        GA = T.GS[:, 32:64]
        ts(GA, T.XH[:, 7::8], -163840.0, 5.0, A.mult, A.add, "XH", "GA")
        op("V", lambda: v.reciprocal(GS, GA), "GA", "GS")
        lastw["gs0"] = lastw["gs1"] = lastw["GS"]
        for k in range(8):
            for s in range(2):
                c = 8 * s + k
                op("V", lambda: v.tensor_reduce(T.RP[:, c:c + 1], T.GS[:, 16 * s:16 * s + 16], X, A.min, negate=True), "gs%d" % s, "rp%d" % c)
            if k == 7:
                break
            for s in range(2):
                c = 8 * s + k
                ts(T.TM[:, 16 * s:16 * s + 16], T.E[:, 128 * s + k:128 * s + 128:8], T.RP[:, c:c + 1], 0.062 * 0.25 ** k, A.min, A.subtract,
                   "E rp%d" % c, "tm%d" % s)
            for s in range(2):
                a = T.GS[:, 16 * s:16 * s + 16]
                tt(a, a, T.TM[:, 16 * s:16 * s + 16], A.max, "gs%d tm%d" % (s, s), "gs%d" % s)
        K = T.KK[:, 0:16]
        tt(K, T.RP[:], T.TK[:], A.is_gt, "TK " + " ".join("rp%d" % c for c in range(16)), "K")
        tt(T.KK[:, 16:32], K, T.SG[:, 0:16], A.mult, "K SG", "KA")
        tt(T.KK[:, 32:48], K, T.SG[:, 16:32], A.mult, "K SG", "KB")
        tt(T.KK[:, 48:64], K, T.SG[:, 32:48], A.mult, "K SG", "KC")
        scan(T.KK[:, 80:96], T.H8[:], T.KK[:, 16:32], 0.0, A.mult, A.add, "H8 KA", "CU")
        for s in range(2):
            op("V", lambda: v.tensor_reduce(T.AL[:, 16 + s:17 + s], T.KK[:, 48 + 8 * s:56 + 8 * s], X, A.add), "KC AL", "al%d" % s)
        tt(T.AL[:, 0:16], T.KK[:, 32:48], T.KK[:, 80:96], A.subtract, "KB CU AL", "al2")
        if t == 0:
            setup_e()
            halves()
        for s in range(2):
            tt(T.INC[:, 256 * s:256 * s + 256], T.AL[:].indirect(T.IL[:, 16 * s:16 * s + 16]), T.RS[:, 774 * s:774 * s + 256], A.add,
               "al0 al1 al2 RS IL0 IL1", "INC%d" % s)
        for s in range(2):
            scan(T.O[:, 256 * s:256 * s + 256], T.INC[:, 256 * s:256 * s + 256], B(s)[:, 0:256], 0.0, A.add, A.max, "INC%d B%d" % (s, s), "O%d" % s)
        for s in range(2):
            for k in range(8):
                n, e, o = 256 >> k, 256 * (8 * s + k + 1), 774 * s + 256 + so[k]
                scan(T.XO[:, e - n:e], T.RS[:, o:o + n], T.O[:, 256 * s + (1 << k) - 1:256 * s + 256:1 << k], -65536.0, A.add, A.max, "RS O%d" % s, "", "XO")
        act(T.KK[:, 64:80], K, "K", "K2", scale=16384.0)
        ts(T.YI[:, 0:16], T.XO[:, 255::256], -1.0, 4096.0, A.mult, A.add, "XO", "Y0")
        ts(T.YI[:, 16:32], T.YI[:, 0:16], 8191, None, A.bitwise_and, None, "Y0", "Y1")
        g0 = 3 * t % 8
        for s in range(2):
            for a, b, c in ((0, 8 - g0, g0), (8 - g0, 8, 0)):
                if a < b:
                    tt(T.YT[:, 16 * s + c:16 * s + c + b - a], T.YI[:, 16 + 8 * s + a:16 + 8 * s + b], T.KK[:, 64 + 8 * s + a:64 + 8 * s + b], A.add, "Y1 K2", "", "YT")
        op("V", lambda: v.transpose(T.YT[:, 32:64], T.YT[:, 0:32]), "YT", "TR")
        LB, lb = T["LB%d" % t], "LB%d" % t
        for q in range(8):
            dma("Y" if q % 2 == 0 else "A", LB[16 * q:16 * q + 16, :], T.YT[q::16, 32:64], "dl%d" % t, "TR", "", lb)
        if t == 0:
            setup_f()
        L = T.LF
        ts(T.DL[:, 0:16], LB[:], 16384.0, None, A.is_lt, None, lb + " DL", "dl")
        ts(T.AI[:, 16:32], LB[:], 8191, None, A.bitwise_and, None, lb, "ai0")
        op("V", lambda: v.transpose(T.DL[:, 32:64], T.DL[:, 0:32]), "dl", "dt")
        ts(T.AI[:, 32:48], T.AI[:, 16:32], 4096, None, A.min, None, "ai0", "ai1")
        scan(T.WC[:, 0:32], T.H10[:, 0:32], T.DL[:, 32:64], 0.0, A.mult, A.add, "H10 dt", "w0")
        tt(T.AI[:, 16:32], T.AI[:, 32:48], T.JL[:, 0:16], A.add, "ai1 JL", "ai0")

        def mean(b):
            b, h = divmod(b, 2)
            o = 256 * b + 128 * h
            tt(T.XW[:, o + 96 * b:o + 96 * b + 128], T.HP[:, 256 * b:256 * b + 256].indirect(T.AU[:, 8 * h:8 * h + 8]),
               T.HP[:, 1024 + o:1152 + o], A.add, "HP AU", "", "XZ%d" % b)
        for i in range(2):
            ts(T.WC[:, 32 + 16 * i:48 + 16 * i], T.WC[:, 0:16], 0.0, T.WC[:, 16 * i + 15:16 * i + 16], A.mult, A.add, "w0", "w%d" % (1 + i))
        ts(T.AI[:, 0:16], T.AI[:, 16:32], 255, None, A.bitwise_and, None, "ai0", "ai")
        op("V", lambda: v.transpose(T.WC[:, 64:128], T.WC[:, 0:64]), "w0 w1 w2", "wt")
        cp(T.AU[:], T.AI[:, 0:16], "ai", "AU")
        act(L[:, 16:32], T.DL[:, 0:16], "dl", "l1", scale=-1024.0)
        JL = T.JL[:, 0:16]
        tt(L[:, 32:48], L[:, 16:32], JL, A.add, "l1 JL", "l2")
        Wi, Cn, Bi = T.WC[:, 64:80], T.WC[:, 96:112], T.WC[:, 128:144]
        scan(Bi, T.NEG[:, 0:16], Cn, 0.0, A.max, A.add, "wt NEG", "bi")
        tt(L[:, 48:64], Wi, Cn, A.subtract, "wt", "l3")
        mean(0)
        tt(L[:, 64:80], L[:, 48:64], Bi, A.add, "l3 bi", "l4")
        mean(1)
        ts(L[:, 80:96], L[:, 64:80], 1.0, T.WC[:, 143:144], A.subtract, A.subtract, "l4 bi", "l5")
        tt(L[:, 96:112], L[:, 32:48], L[:, 64:80], A.subtract, "l2 l4", "l6")
        mean(2)
        tt(L[:, 112:128], L[:, 80:96], L[:, 96:112], A.max, "l5 l6", "l7")
        mean(3)
        ts(T.PU[:], L[:, 112:128], T.WC[:, 143:144], None, A.add, None, "l7 bi", "PU")
        mean(4)
        mean(5)
        op("V", lambda: v.tensor_copy(T.LR[:].indirect(T.PU[:]), T.ICOL[:, 0:256]), "PU ICOL", "LR")
        ts(L[:, 128:144], L[:, 112:128], T.WC[:, 143:144], None, A.add, None, "l7 bi", "pos")
        ts(L[:, 144:160], L[:, 128:144], 96.0, None, A.is_lt, None, "pos", "m0")
        tt(L[:, 160:176], L[:, 128:144], JL, A.subtract, "pos JL", "m1")
        scan(T.LM[:], T.MK[:, 0:96], T.LR[:, 0:96], 0.0, A.add, A.max, "MK LR", "ln")
        ts(L[:, 176:192], L[:, 160:176], 256.0, None, A.add, None, "m1", "m2")
        mean(6)
        mean(7)
        ts(T.LU[:, 0:6], T.LM[:, 15::16], T.MK[:, 111:112], None, A.subtract, None, "ln MK", "LU")
        tt(L[:, 160:176], L[:, 176:192], L[:, 144:160], A.mult, "m2 m0", "m3")
        for b in range(4):
            o, i = T.ET[:, b:384:4], T.XW[:, 352 * b:352 * b + 256].indirect(T.LU[:, 0:6])
            if b in (0, 2):
                op("A", lambda: ac.activation(o, i, AF.Copy), "XZ%d LU" % b, "", "ET")
            else:
                op("V", lambda: v.tensor_copy(o, i), "XZ%d LU" % b, "", "ET")
        quant(T.EQ[:], T.ES[:], T.ET[:], "ET ET4", "EQ ES")
        remote(T["AC%d" % t][:, 0:96].bitcast(dt.uint8), T.EQ[:, 0:96].bitcast(dt.uint8), "ca%d" % t, "lc%d" % t, "EQ", "AC%d" % t)
        remote(T["AS%d" % t][:, 0:96], T.ES[:, 0:96], "ca%d" % t, "lc%d" % t, "ES", "AS%d" % t)
        tt(L[:, 176:192], L[:, 160:176], JL, A.add, "m3 JL", "m2")
        cp(T.SU[:], L[:, 176:192], "m2", "SU")
        if last:
            cp(T.AF[:, 0:16], T.AI[:, 0:16], "ai AF", "af")
            op("V", lambda: v.transpose(T.AF[:, 32:64], T.AF[:, 0:32]), "af", "at")
            for q in range(8):
                p = 32 * (q // 2)
                dma("Y", T.al[q:q + 1, 0:256], T.AF[p:p + 16, 32 + 16 * (q % 2):48 + 16 * (q % 2)], "dout", "at")
            dma("Y", T.al[:, 256:352], T.LR[0::16, 0:96], "dout", "LR")
        AC, AS = T["AC%d" % t], T["AS%d" % t]
        for b in range(4):
            kb = "B%d" % DB[b]
            mm(B(DB[b])[:, 0:128], T.WQ[:, 128 * b:128 * b + 128], T.WS[:, 128 * b:128 * b + 128], AC[:], AS[:], True, False, "WQ WS AC%d AS%d" % (t, t), kb)
            mm(B(DB[b])[:, 0:128], T.ELQ[:, 128 * b:128 * b + 128], T.ELS[:, 128 * b:128 * b + 128], AC[:], AS[:], False, True, "ELQ ELS AC%d AS%d" % (t, t), "", kb)
        for b in range(4):
            kb, o, i = "B%d" % DB[b], T.XW[:, 352 * b + 256:352 * b + 352], B(DB[b])[:, 0:96]
            act(o, i, kb, "XT%d" % b, scale=0.03125)
        for b in range(4):
            o, i = T.XT[:, b::4], T.XW[:, 352 * b:352 * b + 352].indirect(T.SU[:])
            if b == 3:
                o1, o2 = T.XT[:, 3:512:4], T.XT[:, 515::4]
                i1, i2 = [T.XW[:, 1056:1408].indirect(T.SU[:, 8 * h:8 * h + 8]) for h in range(2)]
                op("A", lambda: ac.activation(o1, i1, AF.Copy), "XZ3 XT3 SU", "", "XT")
                op("V", lambda: v.tensor_copy(o2, i2), "XZ3 XT3 SU", "", "XT")
            else:
                op("V", lambda: v.tensor_copy(o, i), "XZ%d XT%d SU" % (b, b), "", "XT")
    quant(T.XQ[:], T.XS[:], T.XT[:], "XT", "XQ0 XQ1")
    dma("Y", T.oc[:], T.XQ[:].bitcast(dt.uint8), "dout", "XQ0 XQ1")
    for k in range(4):
        dma("A", T.osc[4 * k:4 * k + 4, :], T.XS[32 * k:32 * k + 4, :], "dout", "XQ0 XQ1")
    mm(B(3)[:, 0:256], T.VQ[:], T.VS[:], T.XQ[:], T.XS[:], True, True, "VQ VS XQ0 XQ1", "B3")
    cp(T.YO[:], B(3)[:, 0:256], "B3", "YO")
    dma("Y", T.y[:], T.YO[:], "dout", "YO")
    for s in sorted(tot):
        need("G", [(s, tot[s])])
